import numpy as np, ml_dtypes
CORES = [66,74,82,90,194,202,210,218]
N = 8
import mx_ref
BF = ml_dtypes.bfloat16
def f(rng, *shape):
    return mx_ref.flush((rng.standard_normal(shape, dtype=np.float32) * np.exp2(rng.integers(-2, 3, shape[:-1] + (1,)))).astype(BF))
def wide(rng, *shape, cols=0):
    v = rng.standard_normal(shape, dtype=np.float32) * np.exp2(rng.integers(-12, 13, shape)).astype(np.float32)
    if cols: v *= np.repeat(np.exp2(rng.integers(-cols, cols + 1, shape[:-2] + (1, shape[-1] // 4))) * (rng.random(shape[:-2] + (1, shape[-1] // 4)) > 0.0625), 4, axis=-1).astype(np.float32)
    return mx_ref.flush(v.astype(BF))
def cols(t, e):
    v = np.concatenate([t.reshape(128, -1, 4), np.zeros((128, 1, 4), BF)], axis=1)
    return np.ascontiguousarray(v[:, e]).reshape(128, -1)
def tile(rs):
    return np.stack(rs, axis=2).reshape(128, -1).astype(BF)
def cut(t, i, w=512):
    return t[:, w * i:w * i + w]
def decode(q):
    o = []
    for b in range(4):
        e = np.zeros((128, 128, 4), np.float32); e[np.arange(128), np.arange(128), b] = 1
        o.append(mx_ref.matmul(mx_ref.quantize(e.reshape(128, 512).astype(BF)), q))
    return np.stack(o, axis=2).reshape(128, -1)
T, CK = 256, 48
def gates(g):
    t = np.zeros((128, 512), BF); t[:, :4 * N] = g
    return np.stack([t] * N)
def plus(g):
    return np.maximum(np.abs(g.astype(np.float32)), np.float32(0.0625)).astype(BF)
def apart(rng):
    g = np.zeros((128, 4 * N), BF)
    for e in range(N): g[8 * e:8 * e + 8, 4 * e:4 * e + 4] = plus(f(rng, 8, 4))
    return g
def setup_inputs(rng):
    return {"x": f(rng, N, 128, 4 * T), "wg": gates(f(rng, 128, 4 * N)), "w1": f(rng, N, 128, 2048)}
def setup_inputs_alike(rng):
    d = setup_inputs(rng); d["wg"] = gates(np.tile(f(rng, 128, 4), (1, N))); return d
def setup_inputs_ties(rng):
    d = setup_inputs(rng); d["wg"] = gates(plus(f(rng, 128, 4 * N))); d["x"] = -plus(d["x"])
    for s in range(N):
        k = rng.permutation(np.arange(T) // 5 if s % 2 else np.arange(T) % (T // (CK + 1)))
        d["x"][s] = d["x"][s].reshape(128, T, 4)[:, k].reshape(128, -1)
    return d
def setup_inputs_split(rng):
    d = setup_inputs(rng); g = apart(rng)
    v = d["x"].astype(np.float32).reshape(N, 128, T, 4)
    for s in range(N):
        p = rng.permutation(T)
        for e in range(N):
            sign = np.full((1, T, 1), -1, np.float32); sign[:, p[(e * CK + np.arange(CK)) % T]] = 1
            v[s, 8 * e:8 * e + 8] = np.abs(v[s, 8 * e:8 * e + 8]) * sign
    d["x"] = v.reshape(N, 128, 4 * T).astype(BF); d["wg"] = gates(g); return d
def setup_inputs_zeros(rng):
    d = setup_inputs(rng); g = apart(rng)
    v = d["x"].astype(np.float32).reshape(N, 128, T, 4)
    for s in range(N):
        for e in range(N):
            p = rng.permutation(T); u = np.abs(v[s, 8 * e:8 * e + 8])
            u[:, p[CK // 2:CK // 2 + CK]] = np.where(rng.random((8, CK, 4)) < 0.5, np.float32(-0.0), np.float32(0.0))
            u[:, p[CK // 2 + CK:]] *= np.float32(-1)
            v[s, 8 * e:8 * e + 8] = u
    d["x"] = v.reshape(N, 128, 4 * T).astype(BF); d["wg"] = gates(g); return d
def setup_inputs_spread(rng):
    d = setup_inputs(rng); d["x"] = wide(rng, N, 128, 4 * T, cols=6); return d
def check_inputs(d):
    b = []
    g = d["wg"].astype(np.float32)
    if (g != g[0]).any() or (g[:, :, 4 * N:] != 0).any(): b.append("wg")
    return b
def reference(x, wg, w1):
    took = []
    for s in range(N):
        z = mx_ref.matmul(mx_ref.quantize(wg[s]), mx_ref.quantize(x[s])) + np.float32(0.0)
        took.append([np.argsort(-z[e], kind="stable")[:CK] for e in range(N)])
    y = np.zeros((N, 128, T, 4), np.float32)
    for e in range(N):
        q = mx_ref.quantize(np.concatenate([cols(x[s], took[s][e]) for s in range(N)], axis=1))
        rs = [np.maximum(mx_ref.matmul(mx_ref.quantize(np.ascontiguousarray(cut(w1[e], i))), q), np.float32(0.0)) * np.float32(0.05) for i in range(4)]
        v = decode(mx_ref.quantize(tile(rs))).reshape(128, N, CK, 4)
        for s in range(N): y[s][:, took[s][e]] += v[:, s]
    return {"y": y.reshape(N, 128, 4 * T)}

@@ -1,0 +1,338 @@
+from concourse.bass import DstId, RemoteDMATransfer
+from concourse.mybir import dt, AluOpType as A, AxisListType, ActivationFunctionType as F
+
+N, TOK, CK = 8, 256, 48
+B4, B2 = 4 * CK, 2 * CK
+OWN = (N - 1) * CK
+ALLC = (2 * N - 1) * CK
+HALF = 4 * CK
+NE, NV = 3, 3
+ULP = 2.0 ** -24 * (1 + 2.0 ** -6)
+TINY = 2.0 ** -124
+
+SCRATCH = {
+    "xs": ("sbuf", [128, 4 * TOK], "bfloat16"),
+    "xs1": ("sbuf", [128, 4 * TOK + 16], "bfloat16"), "xs2": ("sbuf", [128, 4 * TOK + 16], "bfloat16"),
+    "xs3": ("sbuf", [128, 4 * TOK + 16], "bfloat16"),
+    "wgs": ("sbuf", [128, 32], "bfloat16"),
+    "wr": ("sbuf", [128, 512], "bfloat16"),
+    "w1s": ("sbuf", [128, 2048], "bfloat16"),
+    "qx": ("sbuf", [128, TOK], "float8_e4m3fn_x4"), "sx": ("sbuf", [128, TOK], "uint8"),
+    "qr": ("sbuf", [128, 128], "float8_e4m3fn_x4"), "sr": ("sbuf", [128, 128], "uint8"),
+    "qw": ("sbuf", [128, 512], "float8_e4m3fn_x4"), "sw": ("sbuf", [128, 512], "uint8"),
+    "ones": ("sbuf", [128, 512], "bfloat16"),
+    "em": ("sbuf", [128, 2048], "bfloat16"),
+    "qe": ("sbuf", [128, 512], "float8_e4m3fn_x4"), "se": ("sbuf", [128, 512], "uint8"),
+    "ps": ("psum", [128, 4096], "float32"),
+    "pi": ("sbuf", [128, 4], "int32"), "bi": ("sbuf", [128, 4], "int32"), "bf": ("sbuf", [128, 4], "float32"),
+    "bp": ("sbuf", [128, 4], "float32"),
+    "wgo": ("sbuf", [128, 32], "int32"), "wgu": ("sbuf", [128, 32], "uint16"),
+    "col": ("sbuf", [128, 256], "float32"), "val": ("sbuf", [128, TOK], "float32"),
+    "meq": ("sbuf", [128, 256], "float32"), "mne": ("sbuf", [128, 256], "float32"), "mnb": ("sbuf", [128, 256], "bfloat16"),
+    "idw": ("sbuf", [128, 9 * B2], "float32"),
+    "eix": ("sbuf", [128, 128], "float32"), "gm": ("sbuf", [128, 128], "float32"),
+    "m1": ("sbuf", [128, 256], "float32"), "fs": ("sbuf", [128, 256], "float32"),
+    "ulp": ("sbuf", [128, 256], "float32"), "zz": ("sbuf", [128, 512], "float32"),
+    "eq": ("sbuf", [128, 256], "bfloat16"), "eqs": ("sbuf", [128, 256], "bfloat16"),
+    "cmp": ("sbuf", [128, 16, 264], "bfloat16"), "cv": ("sbuf", [128, NV, 264], "bfloat16"), "acc": ("sbuf", [128, 16], "float32"),
+    "rku": ("sbuf", [128, 16], "uint16"),
+    "wa": ("sbuf", [128, 256], "float32"), "wb": ("sbuf", [128, 3, 32], "float32"), "va": ("sbuf", [128, 96], "float32"),
+    "ca": ("sbuf", [128, 6], "float32"), "oa": ("sbuf", [128, 24], "float32"), "of": ("sbuf", [128, 24], "uint16"),
+    "xt": ("sbuf", [128, 4 * N * CK], "bfloat16"),
+    "sb": ("sbuf", [128, ALLC], "float8_e4m3fn_x4"), "ss": ("sbuf", [128, ALLC], "uint8"),
+    "ht": ("sbuf", [128, 4 * N * CK], "bfloat16"),
+    "rb": ("sbuf", [128, ALLC], "float8_e4m3fn_x4"), "rs": ("sbuf", [128, ALLC], "uint8"),
+    "tk": ("sbuf", [128, 16], "float32"), "pb": ("sbuf", [128, 16], "float32"), "d2": ("sbuf", [128, 32], "float32"),
+    "x1": ("sbuf", [128, 32], "float32"), "yb": ("sbuf", [128, 64], "float32"), "x2": ("sbuf", [128, 64], "float32"),
+    "c2": ("sbuf", [128, 32], "float32"), "tp": ("sbuf", [128, 128], "float32"),
+    "km": ("sbuf", [128, 128], "float32"),
+    "l1": ("sbuf", [128, 64], "float32"), "l2": ("sbuf", [128, 32], "float32"), "l3": ("sbuf", [128, 16], "float32"),
+    "k1": ("sbuf", [128, 64], "float32"), "k2": ("sbuf", [128, 32], "float32"), "k3": ("sbuf", [128, 16], "uint16"),
+    "k4": ("sbuf", [128, 16], "float32"),
+    "row": ("sbuf", [128, 256], "float32"), "wc": ("sbuf", [128, 256], "float32"), "wd": ("sbuf", [128, 3, 32], "float32"),
+    "vc": ("sbuf", [128, 96], "float32"), "cc": ("sbuf", [128, 6], "float32"), "oc": ("sbuf", [128, 24], "float32"),
+    "po": ("sbuf", [128, 48], "uint16"), "lb": ("sbuf", [128, 32], "uint16"),
+    "vv": ("sbuf", [128, N, B4], "float32"),
+    "pp0": ("sbuf", [128, (N + 1) * B2], "float32"), "pp1": ("sbuf", [128, (N + 1) * B2], "float32"),
+    "yo": ("sbuf", [128, 4 * TOK], "float32"),
+}
+SEMAPHORES = ["v", "s", "t", "p", "dwg", "dx", "dxs", "dw1", "dy", "a1A", "a1B", "a2A", "a2B", "loc"]
+
+
+def rank_program(g, core, T, topo):
+    rank = T.rank_of(core)
+    if rank is None:
+        return
+    Q = {"v": g.vector, "s": g.scalar, "t": g.tensor, "p": g, "y": g.sync}
+    cnt = {"v": 0, "s": 0, "t": 0, "p": 0}
+    known = {}
+
+    def need(q, *deps):
+        best = {}
+        for d in deps:
+            if d is None:
+                continue
+            for sem, val in (d if isinstance(d, list) else [d]):
+                best[sem] = max(best.get(sem, 0), val)
+        for sem, val in best.items():
+            if known.get((q, sem), 0) < val:
+                Q[q].wait_ge(T.sem[sem], val)
+                known[(q, sem)] = val
+
+    def run(q, fn, *deps):
+        need(q, *deps)
+        cnt[q] += 1
+        fn().then_inc(T.sem[q], 1)
+        return (q, cnt[q])
+
+    V, S = g.vector, g.scalar
+
+    def cp(q, out, in_, *deps):
+        if q == "v":
+            return run("v", lambda: V.tensor_copy(out, in_), *deps)
+        return run("s", lambda: S.activation(out, in_, F.Copy), *deps)
+
+    def ts(out, in0, s1, op0, *deps):
+        return run("v", lambda: V.tensor_scalar(out, in0, s1, None, op0), *deps)
+
+    def tt(out, a, b, op, *deps):
+        return run("v", lambda: V.tensor_tensor(out, a, b, op), *deps)
+
+    g.sync.dma_start(T.xs[:, :], T.x[:, :]).then_inc(T.sem.dx, 16)
+    g.scalar.dma_start(T.wgs[:, 0:32], T.wg[:, 0:32]).then_inc(T.sem.dwg, 16)
+    g.sync.wait_ge(T.sem.dx, 16)
+    for t in range(1, 4):
+        g.sync.dma_start(T["xs%d" % t][:, 16 - t:16 - t + 4 * TOK], T.x[:, :]).then_inc(T.sem.dxs, 16)
+    g.sync.dma_start(T.w1s[:, :], T.w1[:, :]).then_inc(T.sem.dw1, 16)
+
+    i_pi = run("p", lambda: g.iota(T.pi[:, 0:1], [[0, 1]], 0, 1))
+    i_wgo = run("p", lambda: g.iota(T.wgo[:, :], [[4, 8], [0, 4]], 0, 0))
+    i_col = run("p", lambda: g.iota(T.col[:, :], [[0, 16], [1, 16]], 0, 0, allow_small_or_imprecise_dtypes=True))
+    i_val = run("p", lambda: g.iota(T.val[:, :], [[4, TOK]], 0, 0, allow_small_or_imprecise_dtypes=True))
+    c_one = run("v", lambda: V.memset(T.ones[:, :], 1.0))
+    i_em = None
+    for b in range(4):
+        i_em = run("p", lambda: g.affine_select(T.em[:, 512 * b:512 * b + 512], T.ones[:, :], [[-1, 512]], A.is_equal, 0.0, b, 4), c_one)
+    i_eix = run("p", lambda: g.iota(T.eix[:, :], [[1, 8], [0, 16]], 0, 0, allow_small_or_imprecise_dtypes=True))
+    i_idw = run("p", lambda: g.iota(T.idw[:, :], [[1, 9 * B2]], 0, 0, allow_small_or_imprecise_dtypes=True))
+
+    cb = [ts(T.bi[:, 0:1], T.pi[:, 0:1], 3, A.bitwise_and, i_pi),
+          ts(T.bi[:, 1:2], T.pi[:, 0:1], 15, A.bitwise_and, i_pi),
+          ts(T.bi[:, 2:3], T.pi[:, 0:1], 4, A.arith_shift_right, i_pi)]
+    c_bf = cp("v", T.bf[:, 0:3], T.bi[:, 0:3], cb)
+    c_wgu = ts(T.wgu[:, :], T.wgo[:, :], T.bf[:, 0:1], A.add, i_wgo, c_bf)
+    R = T.bf[:, 1:2]
+    c_meq = ts(T.meq[:, :], T.col[:, :], R, A.is_equal, i_col, c_bf)
+    c_mne = ts(T.mne[:, :], T.col[:, :], R, A.not_equal)
+
+    k_wr = cp("s", T.wr[:, :], T.wgs[:, 0:32].indirect(T.wgu[:, 0:32]), ("dwg", 16), c_wgu)
+    k_qr = run("v", lambda: V.quantize_mx(T.qr[:, :], T.sr[:, :], T.wr[:, :]), k_wr)
+    k_qx = run("v", lambda: V.quantize_mx(T.qx[:, :], T.sx[:, :], T.xs[:, :]), ("dx", 16))
+    Z, Z2 = T.ps[:, 3584:3584 + TOK], T.ps[:, 3072:3072 + TOK]
+    k_z2 = run("t", lambda: g.tensor.matmul_mx(Z2, T.qr[:, :], T.sr[:, :], T.qx[:, :], T.sx[:, :], True, True), k_qr, k_qx)
+    k_z = run("t", lambda: g.tensor.matmul_mx(Z, T.qr[:, :], T.sr[:, :], T.qx[:, :], T.sx[:, :], True, True), k_qr, k_qx)
+    c_mnb = ts(T.mnb[:, :], T.col[:, :], R, A.not_equal)
+
+    k_ulp = run("s", lambda: S.activation(T.ulp[:, :], Z2, F.Abs, bias=TINY, scale=ULP), k_z2)
+    k_zc = cp("s", T.zz[:, 0:256], Z2, k_z2)
+    k_m1 = tt(T.m1[:, :], Z, T.meq[:, :], A.mult, k_z, c_meq)
+    k_zn = tt(T.zz[:, 256:512], Z, T.ulp[:, :], A.add, k_ulp)
+    k_fs = run("v", lambda: V.tensor_tensor_scan(T.fs[:, :], T.mne[:, :], T.m1[:, :], 0.0, A.mult, A.add), k_m1, c_mne)
+    k_eqs, k_ext, k_acc, k_fix = None, None, None, None
+    k_cv = []
+    for i in range(16):
+        own = T.fs[:, 16 * i + 15:16 * i + 16]
+        k = ts(T.cmp[:, i, 0:256], T.zz[:, 16 * i + 16:16 * i + 272], own, A.is_gt, k_fs, k_zc, k_zn)
+        if i < NE:
+            row = T.cmp[:, i, 0:256]
+            k_acc = run("s", lambda: S.activation(row, row, F.Copy, accum_out=T.acc[:, i:i + 1]), k)
+            k_fix = k_acc
+        elif i < 16 - NV:
+            row = T.cmp[:, i, 0:257]
+            k_acc = run("s", lambda: S.activation(row, row, F.Copy, accum_out=T.acc[:, i:i + 1]), k, k_ext)
+        else:
+            k_cv.append((i, k))
+        if i == NE - 2:
+            k_eq = tt(T.eq[:, :], Z, T.fs[:, :], A.is_equal, k_fs)
+        if i == NE - 1:
+            k_eqs = run("v", lambda: V.tensor_tensor_scan(T.eqs[:, :], T.mnb[:, :], T.eq[:, :], 0.0, A.mult, A.subtract), k_eq, c_mnb)
+            k_ext = cp("v", T.cmp[:, NE:16, 256], T.eqs[:, 16 * NE + 15:256:16], k_eqs)
+        if i == NE + 4:
+            k_fix = tt(T.acc[:, 0:NE], T.acc[:, 0:NE], T.eqs[:, 15:16 * NE:16], A.add, k_fix, k_eqs)
+    for j in range(NV):
+        i, k = k_cv[j]
+        k_cv[j] = run("v", lambda: V.tensor_tensor_scan(T.cv[:, j, 0:257], T.ones[:, 0:257], T.cmp[:, i, 0:257], 0.0, A.mult, A.add), k, k_ext, c_one)
+    k_acc = [k_acc, k_fix]
+    k_rku = [cp("v", T.rku[:, 16 - NV:16], T.cv[:, :, 256], k_cv), cp("v", T.rku[:, 0:16 - NV], T.acc[:, 0:16 - NV], k_acc)]
+
+    def spread(C, O, w, kc, pk, qs):
+        ks = []
+        n = 0
+        for q in range(4):
+            for d in (q, q ^ 1):
+                o = 2 * w * (q ^ pk)
+                ks.append(cp(qs[n % len(qs)], O[32 * d:32 * d + 32, o:o + 2 * w], C[32 * q:32 * q + 32, :], kc))
+                n += 1
+        ks2 = list(ks)
+        for h in range(2):
+            o = 4 * w * (h ^ (pk >> 1))
+            ks2.append(cp(qs[h % len(qs)], O[64 * (1 - h):64 * (1 - h) + 64, o:o + 4 * w], O[64 * h:64 * h + 64, o:o + 4 * w], ks))
+        return ks2
+
+    def lists(W, W2, VT, C, O, kw, flip, pk, qs):
+        ks = [cp(qs[h % len(qs)], W2[:, :, 16 * h:16 * h + 16], W[:, 0:CK], kw) for h in range(2)]
+        kt = run("v", lambda: V.transpose(VT[:, :], W2[:, :, :]), ks)
+        kc = [cp(qs[e % len(qs)], C[:, 3 * (e ^ flip):3 * (e ^ flip) + 3], VT[:, 16 * e:96:32], kt) for e in range(2)]
+        return spread(C, O, 3, kc, pk, qs)
+
+    k_wa = cp("v", T.wa[:, 0:256].indirect(T.rku[:, 0:16]), T.val[:, :], k_rku, i_val)
+    k_oa = lists(T.wa, T.wb, T.va, T.ca, T.oa, k_wa, (rank & 1) ^ 1, (rank >> 1) ^ 3, "vs")
+    k_of = cp("v", T.of[:, :], T.oa[:, :], k_oa)
+    win = [T.xs[:, :]] + [T["xs%d" % t][:, 16:16 + 4 * TOK - 3] for t in range(1, 4)]
+    k_q1 = []
+    for c in range(2):
+        ks = []
+        for t in (2, 0, 3, 1):
+            ks.append(cp("vs"[t // 2], T.xt[:, 4 * HALF * c + t:4 * HALF * (c + 1):4], win[t].indirect(T.of[:, 12 * c:12 * c + 12]), k_of,
+                         ("dxs", 48) if t else ("dx", 16)))
+        o = HALF * c
+        k_q1.append(run("v", lambda: V.quantize_mx(T.sb[:, o:o + HALF], T.ss[:, o:o + HALF], T.xt[:, 4 * o:4 * o + 4 * HALF]), ks))
+
+    loc = [0]
+
+    def send(dels, src_col, dst_col, codes, plane, sem):
+        per = 8 // (4 if len(dels) > 2 else len(dels))
+        for view in ("q", "s"):
+            tr = []
+            for j, de in enumerate(dels):
+                dst = T.cores[rank ^ de]
+                eng = topo.engines(core, dst)
+                mask = sum(1 << e for e in eng[j * per:(j + 1) * per])
+                rid, pid = topo.addr(dst, core)
+                a, b = src_col(de), dst_col(de)
+                if view == "q":
+                    sa, da = codes[:, a:a + CK].bitcast(dt.uint8), codes[:, b:b + CK].bitcast(dt.uint8)
+                else:
+                    sa, da = plane[:, a:a + CK], plane[:, b:b + CK]
+                tr.append(RemoteDMATransfer(dst_ids=[DstId(rid=rid, pnc=pid)], dma_engine_mask=mask, remote_sem=T.sem[sem], src=sa, dst=da))
+                loc[0] += per
+            g.remote_dma_fused(tr, local_sem=T.sem.loc)
+        return 2 * per * len(dels)
+
+    FAR, NEAR = (7, 6, 5, 4), (3, 2, 1)
+    out1, in1 = (lambda de: CK * (7 - de)), (lambda de: OWN + CK * de)
+    need("p", k_q1[0])
+    nA = send(FAR, out1, in1, T.sb, T.ss, "a1A")
+    need("p", k_q1[1])
+    nB = send(NEAR, out1, in1, T.sb, T.ss, "a1B")
+
+    k_qw = run("v", lambda: V.quantize_mx(T.qw[:, :], T.sw[:, :], T.w1s[:, :]), ("dw1", 16))
+    k_qe = run("v", lambda: V.quantize_mx(T.qe[:, :], T.se[:, :], T.em[:, :]), i_em)
+    c_bp = run("v", lambda: V.tensor_scalar(T.bp[:, 0:1], T.bf[:, 2:3], float(B2), float(B2), A.mult, A.add), c_bf)
+    k_rk = [cp("v", T.acc[:, 16 - NV:16], T.cv[:, :, 256], k_cv)] + k_acc
+    k_tk = ts(T.tk[:, :], T.acc[:, :], float(CK), A.is_lt, k_rk)
+    k_pb = ts(T.pb[:, :], T.acc[:, :], T.bp[:, 0:1], A.add, c_bp)
+    k = [tt(T.d2[:, 16 * h:16 * h + 16], T.tk[:, :], T.pb[:, :], A.mult, k_tk, k_pb) for h in range(2)]
+    k = run("v", lambda: V.transpose(T.x1[:, :], T.d2[:, :]), k)
+    ks = [cp("vs"[h], T.yb[:, 32 * h + 16 * j:32 * h + 16 * j + 16], T.x1[:, 16 * h:16 * h + 16], k) for h in range(2) for j in range(2)]
+    k = run("v", lambda: V.transpose(T.x2[:, :], T.yb[:, :]), ks)
+    ks = [cp("vs"[h], T.c2[:, 16 * h:16 * h + 16], T.x2[:, 32 * h:32 * h + 16], k) for h in range(2)]
+    k_tp = spread(T.c2, T.tp, 16, ks, 0, "vs")
+    c_pp = [run("v", lambda: V.memset(T["pp%d" % h][:, 0:B2], 0.0)) for h in range(2)]
+    k_gm = ts(T.gm[:, :], T.eix[:, :], T.bf[:, 2:3], A.is_lt, i_eix, c_bf)
+    k_km = tt(T.km[:, :], T.tp[:, :], T.gm[:, :], A.mult, k_tp, k_gm)
+    kl1 = tt(T.l1[:, :], T.tp[:, 0:64], T.tp[:, 64:128], A.max, k_tp)
+    kk1 = tt(T.k1[:, :], T.km[:, 0:64], T.km[:, 64:128], A.max, k_km)
+    kl2 = tt(T.l2[:, :], T.l1[:, 0:32], T.l1[:, 32:64], A.max, kl1)
+    kk2 = tt(T.k2[:, :], T.k1[:, 0:32], T.k1[:, 32:64], A.max, kk1)
+    kl3 = tt(T.l3[:, :], T.l2[:, 0:16], T.l2[:, 16:32], A.max, kl2)
+    kk3 = tt(T.k4[:, :], T.k2[:, 0:16], T.k2[:, 16:32], A.max, kk2)
+    kk4 = cp("v", T.k3[:, :], T.k4[:, :], kk3)
+    k_lb = [ts(T.lb[:, 16 * b:16 * b + 16], T.l3[:, :], float(CK * b), A.add, kl3) for b in range(2)]
+
+    out2, in2 = (lambda de: OWN + CK * de), (lambda de: CK * (7 - de))
+    arr1 = [("a1A", nA), ("a1B", nB)]
+    rb_free = {}
+    k_r = {}
+    for c in range(2):
+        col = OWN + HALF * (1 - c)
+        for i in range(4):
+            bank = 4 * c + i
+            k_r[(c, i)] = run("t", lambda: g.tensor.matmul_mx(T.ps[:, 512 * bank:512 * bank + HALF], T.qw[:, 128 * i:128 * i + 128], T.sw[:, 128 * i:128 * i + 128],
+                                                  T.sb[:, col:col + HALF], T.ss[:, col:col + HALF], True, True),
+                               arr1[c], k_qw, k_q1[1] if c else None, k_rku)
+    k_q2 = []
+    for c in range(2):
+        o = 4 * HALF * (1 - c)
+        ks = []
+        for i in range(4):
+            bank = 4 * c + i
+            out, src = T.ht[:, o + i:o + 4 * HALF:4], T.ps[:, 512 * bank:512 * bank + HALF]
+            if i % 2 == 0:
+                kk = run("s", lambda: S.activation(out, src, F.Relu, scale=0.05), k_r[(c, i)])
+            else:
+                kk = run("v", lambda: V.tensor_scalar(out, src, 0.0, 0.05, A.max, A.mult), k_r[(c, i)])
+            ks.append(kk)
+            rb_free[bank] = kk
+        col = OWN + HALF * (1 - c)
+        k_q2.append(run("v", lambda: V.quantize_mx(T.rb[:, col:col + HALF], T.rs[:, col:col + HALF], T.ht[:, o:o + 4 * HALF]), ks))
+        need("p", k_q2[c])
+        n2 = send((FAR, NEAR)[c], out2, in2, T.rb, T.rs, ("a2A", "a2B")[c])
+        if c == 0:
+            mA = n2
+        else:
+            mB = n2
+
+    k = cp("v", T.row[:, :], T.idw[:, :].indirect(T.k3[:, 0:16]), kk4, i_idw)
+    k_wc = cp("v", T.wc[:, 0:256].indirect(T.rku[:, 0:16]), T.row[:, :], k)
+    k_oc = lists(T.wc, T.wd, T.vc, T.cc, T.oc, k_wc, 0, 0, "vs")
+    k_po = None
+    for b in range(2):
+        for m in range(3):
+            k_po = ts(T.po[:, 3 * b + m:48:6], T.oc[:, m:24:3], float(CK * b), A.add, k_oc)
+
+    arr2 = [("a2A", mA), ("a2B", mB)]
+    k_d = {}
+    for c in range(2):
+        for b in range(4):
+            bank = 4 * c + b
+            k_d[(c, b)] = run("t", lambda: g.tensor.matmul_mx(T.ps[:, 512 * bank:512 * bank + HALF], T.qe[:, 128 * b:128 * b + 128], T.se[:, 128 * b:128 * b + 128],
+                                                  T.rb[:, HALF * c:HALF * c + HALF], T.rs[:, HALF * c:HALF * c + HALF], True, True),
+                               arr2[c], k_qe, rb_free[bank], k_q2[1] if c else None)
+    done = {}
+    nxt = [0]
+    k_p = {}
+    blk = lambda e: e ^ rank ^ 7
+    for c in range(2):
+        exps = sorted(e for e in range(N) if blk(e) // 4 == c)
+        ks, k0 = [], []
+        for b in range(4):
+            q = "sv"[b % 2]
+            o = 512 * (4 * c + b)
+            if 0 in exps:
+                p = B2 + CK * (b % 2)
+                k0.append(cp(q, T["pp%d" % (b // 2)][:, p:p + CK], T.ps[:, o + CK * (blk(0) % 4):o + CK * (blk(0) % 4) + CK], k_d[(c, b)]))
+            ks.append(cp(q, T.vv[:, 4 * c:4 * c + 4, CK * b:CK * b + CK], T.ps[:, o:o + HALF], k_d[(c, b)]))
+        for e in exps:
+            done[e] = [ks[0:2] + k0[0:2], ks[2:4] + k0[2:4]]
+        while nxt[0] in done:
+            e = nxt[0]
+            for h in range(2):
+                P = T["pp%d" % h]
+                if e == 0:
+                    k_p[(0, h)] = done[0][h]
+                else:
+                    k_p[(e, h)] = run("v", lambda: V.tensor_tensor(P[:, B2 * (e + 1):B2 * (e + 2)], P[:, 0:B2 * (e + 1)].indirect(T.po[:, 6 * e:6 * e + 6]),
+                                                                   T.vv[:, blk(e), B2 * h:B2 * h + B2], A.add), k_p[(e - 1, h)], done[e][h], k_po, c_pp)
+            nxt[0] += 1
+    ny = 0
+    for h in range(2):
+        ks = []
+        for b in (0, 2, 1, 3):
+            ks.append(cp("sv"[b // 2], T.yo[:, 512 * h + b:512 * (h + 1):4], T["pp%d" % (b // 2)][:, :].indirect(T.lb[:, 16 * (b % 2) + 8 * h:16 * (b % 2) + 8 * h + 8]),
+                         k_p[(7, b // 2)], k_lb[b % 2]))
+        need("y", ks)
+        g.sync.dma_start(T.y[:, 512 * h:512 * h + 512], T.yo[:, 512 * h:512 * h + 512]).then_inc(T.sem.dy, 16)
+        ny += 16
+    need("y", ("dy", ny))
+    need("p", [("v", cnt["v"]), ("s", cnt["s"]), ("t", cnt["t"]), ("p", cnt["p"]), ("loc", loc[0])])

@@ -3,12 +3,15 @@ from concourse.mybir import dt, AluOpType as A, AxisListType, ActivationFunction
 
 N, TOK, CK = 8, 256, 48
 B4, B2 = 4 * CK, 2 * CK
-OWN = (N - 1) * CK
-ALLC = (2 * N - 1) * CK
-HALF = 4 * CK
-NE, NV = 3, 3
+NA, NB = 4 * CK, 3 * CK
+PAD = 128 - CK
+OWN = NA + NB + PAD
+SBW = OWN + CK + NA + NB
+RBW = 2 * (NA + NB) + CK
+NV, SEG, SH = 9, 258, 16
 ULP = 2.0 ** -24 * (1 + 2.0 ** -6)
 TINY = 2.0 ** -124
+CUT = (10, 0, 5)
 
 SCRATCH = {
     "xs": ("sbuf", [128, 4 * TOK], "bfloat16"),
@@ -20,38 +23,37 @@ SCRATCH = {
     "qx": ("sbuf", [128, TOK], "float8_e4m3fn_x4"), "sx": ("sbuf", [128, TOK], "uint8"),
     "qr": ("sbuf", [128, 128], "float8_e4m3fn_x4"), "sr": ("sbuf", [128, 128], "uint8"),
     "qw": ("sbuf", [128, 512], "float8_e4m3fn_x4"), "sw": ("sbuf", [128, 512], "uint8"),
-    "ones": ("sbuf", [128, 512], "bfloat16"),
+    "msk": ("sbuf", [128, 3 * SEG], "bfloat16"),
     "em": ("sbuf", [128, 2048], "bfloat16"),
     "qe": ("sbuf", [128, 512], "float8_e4m3fn_x4"), "se": ("sbuf", [128, 512], "uint8"),
     "ps": ("psum", [128, 4096], "float32"),
-    "pi": ("sbuf", [128, 4], "int32"), "bi": ("sbuf", [128, 4], "int32"), "bf": ("sbuf", [128, 4], "float32"),
-    "bp": ("sbuf", [128, 4], "float32"),
+    "pi": ("sbuf", [128, 4], "int32"), "bi": ("sbuf", [128, 8], "int32"), "bf": ("sbuf", [128, 8], "float32"),
+    "bp": ("sbuf", [128, 4], "float32"), "selc": ("sbuf", [128, 2], "uint16"),
     "wgo": ("sbuf", [128, 32], "int32"), "wgu": ("sbuf", [128, 32], "uint16"),
-    "col": ("sbuf", [128, 256], "float32"), "val": ("sbuf", [128, TOK], "float32"),
-    "meq": ("sbuf", [128, 256], "float32"), "mne": ("sbuf", [128, 256], "float32"), "mnb": ("sbuf", [128, 256], "bfloat16"),
+    "col": ("sbuf", [128, 256], "bfloat16"), "val": ("sbuf", [128, TOK], "float32"),
+    "meq": ("sbuf", [128, 256], "bfloat16"), "mne": ("sbuf", [128, 256], "bfloat16"),
     "idw": ("sbuf", [128, 9 * B2], "float32"),
     "eix": ("sbuf", [128, 128], "float32"), "gm": ("sbuf", [128, 128], "float32"),
     "m1": ("sbuf", [128, 256], "float32"), "fs": ("sbuf", [128, 256], "float32"),
     "ulp": ("sbuf", [128, 256], "float32"), "zz": ("sbuf", [128, 512], "float32"),
     "eq": ("sbuf", [128, 256], "bfloat16"), "eqs": ("sbuf", [128, 256], "bfloat16"),
-    "cmp": ("sbuf", [128, 16, 264], "bfloat16"), "cv": ("sbuf", [128, NV, 264], "bfloat16"), "acc": ("sbuf", [128, 16], "float32"),
+    "cmv": ("sbuf", [128, NV * SEG], "bfloat16"), "cv": ("sbuf", [128, NV * SEG], "bfloat16"),
+    "cms": ("sbuf", [128, 16 - NV, 264], "bfloat16"), "acc": ("sbuf", [128, 16], "float32"),
     "rku": ("sbuf", [128, 16], "uint16"),
-    "wa": ("sbuf", [128, 256], "float32"), "wb": ("sbuf", [128, 3, 32], "float32"), "va": ("sbuf", [128, 96], "float32"),
-    "ca": ("sbuf", [128, 6], "float32"), "oa": ("sbuf", [128, 24], "float32"), "of": ("sbuf", [128, 24], "uint16"),
-    "xt": ("sbuf", [128, 4 * N * CK], "bfloat16"),
-    "sb": ("sbuf", [128, ALLC], "float8_e4m3fn_x4"), "ss": ("sbuf", [128, ALLC], "uint8"),
+    "wa": ("sbuf", [128, TOK + SH], "float32"), "wb": ("sbuf", [128, 3, 32], "float32"), "va": ("sbuf", [128, 96], "float32"),
+    "oa": ("sbuf", [128, 24], "float32"), "of": ("sbuf", [128, 26], "uint16"),
+    "xt": ("sbuf", [128, 4 * (OWN + CK)], "bfloat16"),
+    "sb": ("sbuf", [128, SBW], "float8_e4m3fn_x4"), "ss": ("sbuf", [128, SBW], "uint8"),
     "ht": ("sbuf", [128, 4 * N * CK], "bfloat16"),
-    "rb": ("sbuf", [128, ALLC], "float8_e4m3fn_x4"), "rs": ("sbuf", [128, ALLC], "uint8"),
+    "rb": ("sbuf", [128, RBW], "float8_e4m3fn_x4"), "rs": ("sbuf", [128, RBW], "uint8"),
     "tk": ("sbuf", [128, 16], "float32"), "pb": ("sbuf", [128, 16], "float32"), "d2": ("sbuf", [128, 32], "float32"),
-    "x1": ("sbuf", [128, 32], "float32"), "yb": ("sbuf", [128, 64], "float32"), "x2": ("sbuf", [128, 64], "float32"),
-    "c2": ("sbuf", [128, 32], "float32"), "tp": ("sbuf", [128, 128], "float32"),
-    "km": ("sbuf", [128, 128], "float32"),
-    "l1": ("sbuf", [128, 64], "float32"), "l2": ("sbuf", [128, 32], "float32"), "l3": ("sbuf", [128, 16], "float32"),
-    "k1": ("sbuf", [128, 64], "float32"), "k2": ("sbuf", [128, 32], "float32"), "k3": ("sbuf", [128, 16], "uint16"),
-    "k4": ("sbuf", [128, 16], "float32"),
-    "row": ("sbuf", [128, 256], "float32"), "wc": ("sbuf", [128, 256], "float32"), "wd": ("sbuf", [128, 3, 32], "float32"),
-    "vc": ("sbuf", [128, 96], "float32"), "cc": ("sbuf", [128, 6], "float32"), "oc": ("sbuf", [128, 24], "float32"),
-    "po": ("sbuf", [128, 48], "uint16"), "lb": ("sbuf", [128, 32], "uint16"),
+    "x1": ("sbuf", [128, 32], "float32"), "yb": ("sbuf", [128, 64], "float32"), "x2": ("sbuf", [128, 2, 32], "float32"),
+    "tp": ("sbuf", [128, 2, 128], "float32"),
+    "l1": ("sbuf", [128, 2, 64], "float32"), "l2": ("sbuf", [128, 2, 32], "float32"), "l3": ("sbuf", [128, 2, 16], "float32"),
+    "k3": ("sbuf", [128, 16], "uint16"), "sel": ("sbuf", [128, 16], "uint16"),
+    "row": ("sbuf", [128, 256], "float32"), "wd": ("sbuf", [128, 96], "float32"),
+    "vc": ("sbuf", [128, 96], "float32"), "oc": ("sbuf", [128, 24], "float32"),
+    "po": ("sbuf", [128, N, 6], "uint16"), "lb": ("sbuf", [128, 32], "uint16"),
     "vv": ("sbuf", [128, N, B4], "float32"),
     "pp0": ("sbuf", [128, (N + 1) * B2], "float32"), "pp1": ("sbuf", [128, (N + 1) * B2], "float32"),
     "yo": ("sbuf", [128, 4 * TOK], "float32"),
@@ -67,13 +69,17 @@ def rank_program(g, core, T, topo):
     cnt = {"v": 0, "s": 0, "t": 0, "p": 0}
     known = {}
 
+    def flat(deps):
+        for d in deps:
+            if isinstance(d, list):
+                yield from flat(d)
+            elif d is not None:
+                yield d
+
     def need(q, *deps):
         best = {}
-        for d in deps:
-            if d is None:
-                continue
-            for sem, val in (d if isinstance(d, list) else [d]):
-                best[sem] = max(best.get(sem, 0), val)
+        for sem, val in flat(deps):
+            best[sem] = max(best.get(sem, 0), val)
         for sem, val in best.items():
             if known.get((q, sem), 0) < val:
                 Q[q].wait_ge(T.sem[sem], val)
@@ -95,8 +101,20 @@ def rank_program(g, core, T, topo):
     def ts(out, in0, s1, op0, *deps):
         return run("v", lambda: V.tensor_scalar(out, in0, s1, None, op0), *deps)
 
+    def ts2(out, in0, s1, op0, s2, op1, *deps):
+        return run("v", lambda: V.tensor_scalar(out, in0, s1, s2, op0, op1), *deps)
+
     def tt(out, a, b, op, *deps):
         return run("v", lambda: V.tensor_tensor(out, a, b, op), *deps)
+
+    def quant(codes, plane, a, n, tile, *deps):
+        return run("v", lambda: V.quantize_mx(codes[:, a:a + n], plane[:, a:a + n], tile), *deps)
+
+    def iota(out, pattern, base):
+        return run("p", lambda: g.iota(out, pattern, base, 0, allow_small_or_imprecise_dtypes=True))
+
+    FIRST = 4 - (rank & 4)
+    STEP = 4 - 2 * FIRST
 
     g.sync.dma_start(T.xs[:, :], T.x[:, :]).then_inc(T.sem.dx, 16)
     g.scalar.dma_start(T.wgs[:, 0:32], T.wg[:, 0:32]).then_inc(T.sem.dwg, 16)
@@ -106,231 +124,240 @@ def rank_program(g, core, T, topo):
     g.sync.dma_start(T.w1s[:, :], T.w1[:, :]).then_inc(T.sem.dw1, 16)
 
     i_pi = run("p", lambda: g.iota(T.pi[:, 0:1], [[0, 1]], 0, 1))
-    i_wgo = run("p", lambda: g.iota(T.wgo[:, :], [[4, 8], [0, 4]], 0, 0))
-    i_col = run("p", lambda: g.iota(T.col[:, :], [[0, 16], [1, 16]], 0, 0, allow_small_or_imprecise_dtypes=True))
-    i_val = run("p", lambda: g.iota(T.val[:, :], [[4, TOK]], 0, 0, allow_small_or_imprecise_dtypes=True))
-    c_one = run("v", lambda: V.memset(T.ones[:, :], 1.0))
+    i_wgo = run("p", lambda: g.iota(T.wgo[:, :], [[4, 4], [4 * STEP, 2], [0, 4]], 4 * FIRST, 0))
+    i_col = iota(T.col[:, :], [[0, 16], [1, 16]], 0)
+    i_val = iota(T.val[:, :], [[4, TOK]], 0)
+    c_msk = run("v", lambda: V.memset(T.msk[:, :], 1.0))
+    PI = T.pi[:, 0:1]
+    cb = [ts(T.bi[:, 0:1], PI, 3, A.bitwise_and, i_pi), ts(T.bi[:, 1:2], PI, 15, A.bitwise_and), ts(T.bi[:, 2:3], PI, 5, A.arith_shift_right),
+          ts(T.bi[:, 3:4], PI, 16, A.bitwise_and), ts2(T.bi[:, 4:5], PI, 15, A.bitwise_and, 1, A.arith_shift_right)]
+    c_msk = run("v", lambda: V.memset(T.msk[:, 0:3 * SEG:SEG], 0.0), c_msk)
+    c_bf = cp("v", T.bf[:, 0:5], T.bi[:, 0:5], cb)
     i_em = None
     for b in range(4):
-        i_em = run("p", lambda: g.affine_select(T.em[:, 512 * b:512 * b + 512], T.ones[:, :], [[-1, 512]], A.is_equal, 0.0, b, 4), c_one)
-    i_eix = run("p", lambda: g.iota(T.eix[:, :], [[1, 8], [0, 16]], 0, 0, allow_small_or_imprecise_dtypes=True))
-    i_idw = run("p", lambda: g.iota(T.idw[:, :], [[1, 9 * B2]], 0, 0, allow_small_or_imprecise_dtypes=True))
+        s = 2 if b == 1 else 1
+        i_em = run("p", lambda: g.affine_select(T.em[:, 512 * b:512 * b + 512], T.msk[:, s:s + 512], [[-1, 512]], A.is_equal, 0.0, b, 4), c_msk)
+    i_eix = iota(T.eix[:, :], [[1, 4], [STEP, 2], [0, 16]], 0)
+    i_idw = iota(T.idw[:, :], [[1, 9 * B2]], 0)
 
-    cb = [ts(T.bi[:, 0:1], T.pi[:, 0:1], 3, A.bitwise_and, i_pi),
-          ts(T.bi[:, 1:2], T.pi[:, 0:1], 15, A.bitwise_and, i_pi),
-          ts(T.bi[:, 2:3], T.pi[:, 0:1], 4, A.arith_shift_right, i_pi)]
-    c_bf = cp("v", T.bf[:, 0:3], T.bi[:, 0:3], cb)
+    c_pad = run("v", lambda: V.memset(T.cmv[:, SEG - 1:NV * SEG:SEG], 0.0))
     c_wgu = ts(T.wgu[:, :], T.wgo[:, :], T.bf[:, 0:1], A.add, i_wgo, c_bf)
-    R = T.bf[:, 1:2]
-    c_meq = ts(T.meq[:, :], T.col[:, :], R, A.is_equal, i_col, c_bf)
+    R, H16 = T.bf[:, 1:2], T.bf[:, 3:4]
+    c_e = ts2(T.bp[:, 0:1], H16, STEP / 16, A.mult, T.bf[:, 2:3], A.add)
+    c_sel = ts2(T.bp[:, 1:2], T.bf[:, 4:5], 2.0, A.min, 32.0, A.mult)
+    c_meq = ts(T.meq[:, :], T.col[:, :], R, A.is_equal, i_col)
     c_mne = ts(T.mne[:, :], T.col[:, :], R, A.not_equal)
+    c_bp = ts2(T.bp[:, 2:3], T.bp[:, 0:1], float(B2), A.mult, float(B2 * (1 + FIRST) - SH), A.add, c_e)
+    c_sel = ts(T.selc[:, 0:1], T.bp[:, 1:2], H16, A.add, c_sel)
 
-    k_wr = cp("s", T.wr[:, :], T.wgs[:, 0:32].indirect(T.wgu[:, 0:32]), ("dwg", 16), c_wgu)
-    k_qr = run("v", lambda: V.quantize_mx(T.qr[:, :], T.sr[:, :], T.wr[:, :]), k_wr)
-    k_qx = run("v", lambda: V.quantize_mx(T.qx[:, :], T.sx[:, :], T.xs[:, :]), ("dx", 16))
+    k_wr = [cp("sv"[h], T.wr[:, 256 * h:256 * h + 256], T.wgs[:, 0:32].indirect(T.wgu[:, 16 * h:16 * h + 16]), ("dwg", 16), c_wgu) for h in range(2)]
+    k_qr = quant(T.qr, T.sr, 0, 128, T.wr[:, :], k_wr)
+    k_qx = quant(T.qx, T.sx, 0, TOK, T.xs[:, :], ("dx", 16))
     Z, Z2 = T.ps[:, 3584:3584 + TOK], T.ps[:, 3072:3072 + TOK]
     k_z2 = run("t", lambda: g.tensor.matmul_mx(Z2, T.qr[:, :], T.sr[:, :], T.qx[:, :], T.sx[:, :], True, True), k_qr, k_qx)
     k_z = run("t", lambda: g.tensor.matmul_mx(Z, T.qr[:, :], T.sr[:, :], T.qx[:, :], T.sx[:, :], True, True), k_qr, k_qx)
-    c_mnb = ts(T.mnb[:, :], T.col[:, :], R, A.not_equal)
+    c_pp = [run("v", lambda: V.memset(T["pp%d" % h][:, 0:B2], 0.0)) for h in range(2)]
+    c_xt = run("v", lambda: V.memset(T.xt[:, 4 * (NA + NB):4 * OWN], 0.0))
 
     k_ulp = run("s", lambda: S.activation(T.ulp[:, :], Z2, F.Abs, bias=TINY, scale=ULP), k_z2)
     k_zc = cp("s", T.zz[:, 0:256], Z2, k_z2)
     k_m1 = tt(T.m1[:, :], Z, T.meq[:, :], A.mult, k_z, c_meq)
     k_zn = tt(T.zz[:, 256:512], Z, T.ulp[:, :], A.add, k_ulp)
     k_fs = run("v", lambda: V.tensor_tensor_scan(T.fs[:, :], T.mne[:, :], T.m1[:, :], 0.0, A.mult, A.add), k_m1, c_mne)
-    k_eqs, k_ext, k_acc, k_fix = None, None, None, None
-    k_cv = []
-    for i in range(16):
-        own = T.fs[:, 16 * i + 15:16 * i + 16]
-        k = ts(T.cmp[:, i, 0:256], T.zz[:, 16 * i + 16:16 * i + 272], own, A.is_gt, k_fs, k_zc, k_zn)
-        if i < NE:
-            row = T.cmp[:, i, 0:256]
-            k_acc = run("s", lambda: S.activation(row, row, F.Copy, accum_out=T.acc[:, i:i + 1]), k)
-            k_fix = k_acc
-        elif i < 16 - NV:
-            row = T.cmp[:, i, 0:257]
-            k_acc = run("s", lambda: S.activation(row, row, F.Copy, accum_out=T.acc[:, i:i + 1]), k, k_ext)
-        else:
-            k_cv.append((i, k))
-        if i == NE - 2:
-            k_eq = tt(T.eq[:, :], Z, T.fs[:, :], A.is_equal, k_fs)
-        if i == NE - 1:
-            k_eqs = run("v", lambda: V.tensor_tensor_scan(T.eqs[:, :], T.mnb[:, :], T.eq[:, :], 0.0, A.mult, A.subtract), k_eq, c_mnb)
-            k_ext = cp("v", T.cmp[:, NE:16, 256], T.eqs[:, 16 * NE + 15:256:16], k_eqs)
-        if i == NE + 4:
-            k_fix = tt(T.acc[:, 0:NE], T.acc[:, 0:NE], T.eqs[:, 15:16 * NE:16], A.add, k_fix, k_eqs)
-    for j in range(NV):
-        i, k = k_cv[j]
-        k_cv[j] = run("v", lambda: V.tensor_tensor_scan(T.cv[:, j, 0:257], T.ones[:, 0:257], T.cmp[:, i, 0:257], 0.0, A.mult, A.add), k, k_ext, c_one)
-    k_acc = [k_acc, k_fix]
-    k_rku = [cp("v", T.rku[:, 16 - NV:16], T.cv[:, :, 256], k_cv), cp("v", T.rku[:, 0:16 - NV], T.acc[:, 0:16 - NV], k_acc)]
+    own = lambda i: T.fs[:, 16 * i + 15:16 * i + 16]
+    window = lambda i: T.zz[:, 16 * i + 16:16 * i + 272]
+    k_cmp, k_cv, k_ext = [], [], []
 
-    def spread(C, O, w, kc, pk, qs):
-        ks = []
-        n = 0
-        for q in range(4):
-            for d in (q, q ^ 1):
-                o = 2 * w * (q ^ pk)
-                ks.append(cp(qs[n % len(qs)], O[32 * d:32 * d + 32, o:o + 2 * w], C[32 * q:32 * q + 32, :], kc))
-                n += 1
-        ks2 = list(ks)
+    def count(c):
+        o = 3 * SEG * c
+        k_cv.append(run("v", lambda: V.tensor_tensor_scan(T.cv[:, o:o + 3 * SEG], T.msk[:, :], T.cmv[:, o:o + 3 * SEG], 0.0, A.mult, A.add),
+                        k_cmp[3 * c + 2], k_ext, c_pad, c_msk))
+
+    for i in range(NV):
+        k_cmp.append(ts(T.cmv[:, SEG * i:SEG * i + 256], window(i), own(i), A.is_gt, k_fs, k_zc, k_zn))
+        if i == 0:
+            k_eq = tt(T.eq[:, :], Z, T.fs[:, :], A.is_equal)
+        if i == 1:
+            k_eqs = run("v", lambda: V.tensor_tensor_scan(T.eqs[:, :], T.mne[:, :], T.eq[:, :], 0.0, A.mult, A.subtract), k_eq)
+        if i == 2:
+            k_exs = ts2(T.cms[:, :, 256], T.eqs[:, 16 * NV + 15:256:16], -1.0, A.mult, -float(SH), A.add, k_eqs)
+            k_ext.append(cp("v", T.cmv[:, 256:NV * SEG:SEG], T.eqs[:, 15:16 * NV:16]))
+        if i == 4:
+            count(0)
+            k_last = ts2(T.cms[:, 15 - NV, 0:256], window(15), own(15), A.is_gt, -1.0, A.mult)
+    count(1)
+    count(2)
+    k_sg, k_acc = [], None
+    NS = 16 - NV
+    for j in range(NS - 1):
+        k_sg.append(run("s", lambda: S.activation(T.cms[:, j, 0:256], window(NV + j), F.Sign, bias=own(NV + j), scale=-1.0), k_fs, k_zc, k_zn))
+    k_sg.append(k_last)
+    for j in range(NS):
+        row = T.cms[:, j, 0:257]
+        k_acc = run("s", lambda: S.activation(row, row, F.Relu, scale=-1.0, accum_out=T.acc[:, NV + j:NV + j + 1]), k_sg[j], k_exs)
+    k_rku = [cp("v", T.rku[:, NV:16], T.acc[:, NV:16], k_acc), ts(T.rku[:, 0:NV], T.cv[:, 256:NV * SEG:SEG], float(SH), A.add, k_cv)]
+
+    def spread(src, O, w, pk, kc):
+        ks = [[], []]
+        for j in range(4):
+            for h in range(2):
+                q = 2 * h + j // 2
+                d, o = q ^ (j & 1), w * (q ^ pk)
+                ks[h].append(cp("vs"[h], O(32 * d, 32, o, w), src(q), kc))
+            yield
         for h in range(2):
-            o = 4 * w * (h ^ (pk >> 1))
-            ks2.append(cp(qs[h % len(qs)], O[64 * (1 - h):64 * (1 - h) + 64, o:o + 4 * w], O[64 * h:64 * h + 64, o:o + 4 * w], ks))
-        return ks2
+            o = 2 * w * (h ^ (pk >> 1))
+            ks[h].append(cp("vs"[h], O(64 * (1 - h), 64, o, 2 * w), O(64 * h, 64, o, 2 * w), ks[h]))
+        yield ks
 
-    def lists(W, W2, VT, C, O, kw, flip, pk, qs):
-        ks = [cp(qs[h % len(qs)], W2[:, :, 16 * h:16 * h + 16], W[:, 0:CK], kw) for h in range(2)]
-        kt = run("v", lambda: V.transpose(VT[:, :], W2[:, :, :]), ks)
-        kc = [cp(qs[e % len(qs)], C[:, 3 * (e ^ flip):3 * (e ^ flip) + 3], VT[:, 16 * e:96:32], kt) for e in range(2)]
-        return spread(C, O, 3, kc, pk, qs)
-
-    k_wa = cp("v", T.wa[:, 0:256].indirect(T.rku[:, 0:16]), T.val[:, :], k_rku, i_val)
-    k_oa = lists(T.wa, T.wb, T.va, T.ca, T.oa, k_wa, (rank & 1) ^ 1, (rank >> 1) ^ 3, "vs")
-    k_of = cp("v", T.of[:, :], T.oa[:, :], k_oa)
+    k_wa = cp("v", T.wa[:, :].indirect(T.rku[:, 0:16]), T.val[:, :], k_rku, i_val)
+    ks = [cp("vs"[h], T.wb[:, :, 16 * h:16 * h + 16], T.wa[:, SH:SH + CK], k_wa) for h in range(2)]
+    k_va = run("v", lambda: V.transpose(T.va[:, :], T.wb[:, :, :]), ks)
+    k_oa = list(spread(lambda q: T.va[32 * q:32 * q + 32, 0:96:16], lambda p, n, o, w: T.oa[p:p + n, o:o + w], 6, (rank & 3) ^ 3, k_va))[-1]
+    k_of = [cp("v", T.of[:, 0:12], T.oa[:, 0:24:2], k_oa), cp("v", T.of[:, 12:21], T.oa[:, 1:18:2])]
     win = [T.xs[:, :]] + [T["xs%d" % t][:, 16:16 + 4 * TOK - 3] for t in range(1, 4)]
-    k_q1 = []
-    for c in range(2):
-        ks = []
-        for t in (2, 0, 3, 1):
-            ks.append(cp("vs"[t // 2], T.xt[:, 4 * HALF * c + t:4 * HALF * (c + 1):4], win[t].indirect(T.of[:, 12 * c:12 * c + 12]), k_of,
-                         ("dxs", 48) if t else ("dx", 16)))
-        o = HALF * c
-        k_q1.append(run("v", lambda: V.quantize_mx(T.sb[:, o:o + HALF], T.ss[:, o:o + HALF], T.xt[:, 4 * o:4 * o + 4 * HALF]), ks))
+
+    def gather(a, n, o, k):
+        return [cp("vs"[t // 2], T.xt[:, 4 * a + t:4 * (a + n):4], win[t].indirect(T.of[:, o:o + n // 16]), k, ("dxs", 48) if t else ("dx", 16))
+                for t in (2, 0, 3, 1)]
 
     loc = [0]
 
     def send(dels, src_col, dst_col, codes, plane, sem):
-        per = 8 // (4 if len(dels) > 2 else len(dels))
         for view in ("q", "s"):
             tr = []
+            per = [2, 2, 2, 2] if len(dels) == 4 else ([4, 2, 2] if view == "q" else [2, 2, 4])
             for j, de in enumerate(dels):
                 dst = T.cores[rank ^ de]
                 eng = topo.engines(core, dst)
-                mask = sum(1 << e for e in eng[j * per:(j + 1) * per])
+                mask = sum(1 << e for e in eng[sum(per[:j]):sum(per[:j + 1])])
                 rid, pid = topo.addr(dst, core)
-                a, b = src_col(de), dst_col(de)
+                a, b = src_col + CK * j, dst_col + CK * j
                 if view == "q":
                     sa, da = codes[:, a:a + CK].bitcast(dt.uint8), codes[:, b:b + CK].bitcast(dt.uint8)
                 else:
                     sa, da = plane[:, a:a + CK], plane[:, b:b + CK]
                 tr.append(RemoteDMATransfer(dst_ids=[DstId(rid=rid, pnc=pid)], dma_engine_mask=mask, remote_sem=T.sem[sem], src=sa, dst=da))
-                loc[0] += per
+                loc[0] += per[j]
             g.remote_dma_fused(tr, local_sem=T.sem.loc)
-        return 2 * per * len(dels)
+        return (sem, 16)
 
     FAR, NEAR = (7, 6, 5, 4), (3, 2, 1)
-    out1, in1 = (lambda de: CK * (7 - de)), (lambda de: OWN + CK * de)
-    need("p", k_q1[0])
-    nA = send(FAR, out1, in1, T.sb, T.ss, "a1A")
-    need("p", k_q1[1])
-    nB = send(NEAR, out1, in1, T.sb, T.ss, "a1B")
+    need("p", quant(T.sb, T.ss, 0, NA, T.xt[:, 0:4 * NA], gather(0, NA, 0, k_of[0])))
+    arr1 = [send(FAR, 0, OWN + CK, T.sb, T.ss, "a1A")]
+    need("p", quant(T.sb, T.ss, NA, NB, T.xt[:, 4 * NA:4 * (NA + NB)], gather(NA, NB, 12, k_of[1])))
+    arr1.append(send(NEAR, NA, OWN + CK + NA, T.sb, T.ss, "a1B"))
+    k = cp("v", T.of[:, 22:25], T.oa[:, 19:24:2])
+    k_qw = quant(T.qw, T.sw, 0, 512, T.w1s[:, :], ("dw1", 16))
+    k_own = gather(OWN, CK, 22, k)
 
-    k_qw = run("v", lambda: V.quantize_mx(T.qw[:, :], T.sw[:, :], T.w1s[:, :]), ("dw1", 16))
-    k_qe = run("v", lambda: V.quantize_mx(T.qe[:, :], T.se[:, :], T.em[:, :]), i_em)
-    c_bp = run("v", lambda: V.tensor_scalar(T.bp[:, 0:1], T.bf[:, 2:3], float(B2), float(B2), A.mult, A.add), c_bf)
-    k_rk = [cp("v", T.acc[:, 16 - NV:16], T.cv[:, :, 256], k_cv)] + k_acc
-    k_tk = ts(T.tk[:, :], T.acc[:, :], float(CK), A.is_lt, k_rk)
-    k_pb = ts(T.pb[:, :], T.acc[:, :], T.bp[:, 0:1], A.add, c_bp)
-    k = [tt(T.d2[:, 16 * h:16 * h + 16], T.tk[:, :], T.pb[:, :], A.mult, k_tk, k_pb) for h in range(2)]
-    k = run("v", lambda: V.transpose(T.x1[:, :], T.d2[:, :]), k)
-    ks = [cp("vs"[h], T.yb[:, 32 * h + 16 * j:32 * h + 16 * j + 16], T.x1[:, 16 * h:16 * h + 16], k) for h in range(2) for j in range(2)]
-    k = run("v", lambda: V.transpose(T.x2[:, :], T.yb[:, :]), ks)
-    ks = [cp("vs"[h], T.c2[:, 16 * h:16 * h + 16], T.x2[:, 32 * h:32 * h + 16], k) for h in range(2)]
-    k_tp = spread(T.c2, T.tp, 16, ks, 0, "vs")
-    c_pp = [run("v", lambda: V.memset(T["pp%d" % h][:, 0:B2], 0.0)) for h in range(2)]
-    k_gm = ts(T.gm[:, :], T.eix[:, :], T.bf[:, 2:3], A.is_lt, i_eix, c_bf)
-    k_km = tt(T.km[:, :], T.tp[:, :], T.gm[:, :], A.mult, k_tp, k_gm)
-    kl1 = tt(T.l1[:, :], T.tp[:, 0:64], T.tp[:, 64:128], A.max, k_tp)
-    kk1 = tt(T.k1[:, :], T.km[:, 0:64], T.km[:, 64:128], A.max, k_km)
-    kl2 = tt(T.l2[:, :], T.l1[:, 0:32], T.l1[:, 32:64], A.max, kl1)
-    kk2 = tt(T.k2[:, :], T.k1[:, 0:32], T.k1[:, 32:64], A.max, kk1)
-    kl3 = tt(T.l3[:, :], T.l2[:, 0:16], T.l2[:, 16:32], A.max, kl2)
-    kk3 = tt(T.k4[:, :], T.k2[:, 0:16], T.k2[:, 16:32], A.max, kk2)
-    kk4 = cp("v", T.k3[:, :], T.k4[:, :], kk3)
-    k_lb = [ts(T.lb[:, 16 * b:16 * b + 16], T.l3[:, :], float(CK * b), A.add, kl3) for b in range(2)]
+    K = {}
 
-    out2, in2 = (lambda de: OWN + CK * de), (lambda de: CK * (7 - de))
-    arr1 = [("a1A", nA), ("a1B", nB)]
-    rb_free = {}
-    k_r = {}
+    def combine_lists():
+        k_tk = ts(T.tk[:, :], T.rku[:, :], float(CK + SH), A.is_lt, k_rku)
+        k_pb = ts(T.pb[:, :], T.rku[:, :], T.bp[:, 2:3], A.add, c_bp)
+        K["own"] = quant(T.sb, T.ss, NA + NB, 128, T.xt[:, 4 * (NA + NB):4 * (OWN + CK)], k_own, c_xt)
+        k = [tt(T.d2[:, 16 * h:16 * h + 16], T.tk[:, :], T.pb[:, :], A.mult, k_tk, k_pb) for h in range(2)]
+        k_gm = ts(T.gm[:, :], T.eix[:, :], T.bp[:, 0:1], A.is_lt, i_eix, c_e)
+        yield
+        k = run("v", lambda: V.transpose(T.x1[:, :], T.d2[:, :]), k)
+        k_sel = ts(T.sel[:, :], T.va[:, :].indirect(T.selc[:, 0:1]), 0.25, A.mult, c_sel)
+        yield
+        k = [cp("vs"[h], T.yb[:, 32 * h + 16 * j:32 * h + 16 * j + 16], T.x1[:, 16 * h:16 * h + 16], k) for h in range(2) for j in range(2)]
+        yield
+        k = run("v", lambda: V.transpose(T.x2[:, :, :], T.yb[:, :]), k)
+        yield
+        for k in spread(lambda q: T.x2[32 * q:32 * q + 32, :, 0:16], lambda p, n, o, w: T.tp[p:p + n, 0, o:o + w], 32, 0, k):
+            yield
+        k = tt(T.tp[:, 1, :], T.tp[:, 0, :], T.gm[:, :], A.mult, k, k_gm)
+        yield
+        for a, b, w in ((T.tp, T.l1, 64), (T.l1, T.l2, 32), (T.l2, T.l3, 16)):
+            k = tt(b[:, :, :], a[:, :, 0:w], a[:, :, w:2 * w], A.max, k)
+            yield
+        k3 = cp("v", T.k3[:, :], T.l3[:, 1, :], k)
+        K["lb"] = [ts(T.lb[:, 16 * b:16 * b + 16], T.l3[:, 0, :], float(CK * b), A.add) for b in range(2)]
+        yield
+        k = cp("s", T.row[:, :], T.idw[:, :].indirect(T.k3[:, :]), k3, i_idw)
+        yield
+        k = cp("s", T.wd[:, :], T.row[:, :].indirect(T.sel[:, 0:6]), k, k_sel)
+        yield
+        k = run("v", lambda: V.transpose(T.vc[:, :], T.wd[:, :]), k)
+        yield
+        for k in spread(lambda q: T.vc[32 * q:32 * q + 32, 0:96:16], lambda p, n, o, w: T.oc[p:p + n, o:o + w], 6, 0, k):
+            yield
+        K["po"] = [ts(T.po[:, e:e + 4, 3 * b:3 * b + 3], T.oc[:, h:24:2], float(CK * b), A.add, k)
+                   for h, e in ((0, FIRST), (1, FIRST + STEP)) for b in range(2)]
+
+    steps = combine_lists()
+
+    def advance(n):
+        for _ in range(n):
+            next(steps, None)
+
+    chunk1 = ((OWN, CK + NA), (OWN + CK + NA, NB))
+    chunk2 = ((NA, CK + NA), (2 * NA + CK, NB))
+    free, arr2, k_q2 = {}, [], []
     for c in range(2):
-        col = OWN + HALF * (1 - c)
-        for i in range(4):
-            bank = 4 * c + i
-            k_r[(c, i)] = run("t", lambda: g.tensor.matmul_mx(T.ps[:, 512 * bank:512 * bank + HALF], T.qw[:, 128 * i:128 * i + 128], T.sw[:, 128 * i:128 * i + 128],
-                                                  T.sb[:, col:col + HALF], T.ss[:, col:col + HALF], True, True),
-                               arr1[c], k_qw, k_q1[1] if c else None, k_rku)
-    k_q2 = []
-    for c in range(2):
-        o = 4 * HALF * (1 - c)
+        advance(CUT[c])
+        (a, n), o = chunk1[c], 4 * (CK + NA) * c
         ks = []
         for i in range(4):
-            bank = 4 * c + i
-            out, src = T.ht[:, o + i:o + 4 * HALF:4], T.ps[:, 512 * bank:512 * bank + HALF]
+            src = T.ps[:, 512 * (4 * c + i):512 * (4 * c + i) + n]
+            k = run("t", lambda: g.tensor.matmul_mx(src, T.qw[:, 128 * i:128 * i + 128], T.sw[:, 128 * i:128 * i + 128],
+                                                    T.sb[:, a:a + n], T.ss[:, a:a + n], True, True), arr1[c], k_qw, K["own"], k_rku)
+            out = T.ht[:, o + i:o + 4 * n:4]
             if i % 2 == 0:
-                kk = run("s", lambda: S.activation(out, src, F.Relu, scale=0.05), k_r[(c, i)])
+                ks.append(run("s", lambda: S.activation(out, src, F.Relu, scale=0.05), k))
             else:
-                kk = run("v", lambda: V.tensor_scalar(out, src, 0.0, 0.05, A.max, A.mult), k_r[(c, i)])
-            ks.append(kk)
-            rb_free[bank] = kk
-        col = OWN + HALF * (1 - c)
-        k_q2.append(run("v", lambda: V.quantize_mx(T.rb[:, col:col + HALF], T.rs[:, col:col + HALF], T.ht[:, o:o + 4 * HALF]), ks))
+                ks.append(ts2(out, src, 0.0, A.max, 0.05, A.mult, k))
+            free[4 * c + i] = ks[i]
+        k_q2.append(quant(T.rb, T.rs, chunk2[c][0], n, T.ht[:, o:o + 4 * n], ks))
         need("p", k_q2[c])
-        n2 = send((FAR, NEAR)[c], out2, in2, T.rb, T.rs, ("a2A", "a2B")[c])
         if c == 0:
-            mA = n2
+            arr2.append(send(FAR, NA + CK, 0, T.rb, T.rs, "a2A"))
         else:
-            mB = n2
+            arr2.append(send(NEAR, 2 * NA + CK, RBW - NB, T.rb, T.rs, "a2B"))
+    advance(CUT[2])
+    k_qe = quant(T.qe, T.se, 0, 512, T.em[:, :], i_em)
+    advance(99)
 
-    k = cp("v", T.row[:, :], T.idw[:, :].indirect(T.k3[:, 0:16]), kk4, i_idw)
-    k_wc = cp("v", T.wc[:, 0:256].indirect(T.rku[:, 0:16]), T.row[:, :], k)
-    k_oc = lists(T.wc, T.wd, T.vc, T.cc, T.oc, k_wc, 0, 0, "vs")
-    k_po = None
-    for b in range(2):
-        for m in range(3):
-            k_po = ts(T.po[:, 3 * b + m:48:6], T.oc[:, m:24:3], float(CK * b), A.add, k_oc)
-
-    arr2 = [("a2A", mA), ("a2B", mB)]
-    k_d = {}
+    chunk3 = ((0, NA + CK), (RBW - NB, NB))
+    order = [rank ^ de for de in FAR + (0,) + NEAR]
+    done, k_p, nxt = {}, {}, 0
     for c in range(2):
+        a, n = chunk3[c]
+        lo = 5 * c
+        exps = order[lo:lo + n // CK]
+        ks = []
         for b in range(4):
-            bank = 4 * c + b
-            k_d[(c, b)] = run("t", lambda: g.tensor.matmul_mx(T.ps[:, 512 * bank:512 * bank + HALF], T.qe[:, 128 * b:128 * b + 128], T.se[:, 128 * b:128 * b + 128],
-                                                  T.rb[:, HALF * c:HALF * c + HALF], T.rs[:, HALF * c:HALF * c + HALF], True, True),
-                               arr2[c], k_qe, rb_free[bank], k_q2[1] if c else None)
-    done = {}
-    nxt = [0]
-    k_p = {}
-    blk = lambda e: e ^ rank ^ 7
-    for c in range(2):
-        exps = sorted(e for e in range(N) if blk(e) // 4 == c)
-        ks, k0 = [], []
-        for b in range(4):
-            q = "sv"[b % 2]
             o = 512 * (4 * c + b)
+            k = run("t", lambda: g.tensor.matmul_mx(T.ps[:, o:o + n], T.qe[:, 128 * b:128 * b + 128], T.se[:, 128 * b:128 * b + 128],
+                                                    T.rb[:, a:a + n], T.rs[:, a:a + n], True, True), arr2[c], k_qe, free[4 * c + b], k_q2[0])
+            q = "svss"[b]
+            kb = []
             if 0 in exps:
-                p = B2 + CK * (b % 2)
-                k0.append(cp(q, T["pp%d" % (b // 2)][:, p:p + CK], T.ps[:, o + CK * (blk(0) % 4):o + CK * (blk(0) % 4) + CK], k_d[(c, b)]))
-            ks.append(cp(q, T.vv[:, 4 * c:4 * c + 4, CK * b:CK * b + CK], T.ps[:, o:o + HALF], k_d[(c, b)]))
+                p, s = B2 + CK * (b % 2), o + CK * exps.index(0)
+                kb.append(cp(q, T["pp%d" % (b // 2)][:, p:p + CK], T.ps[:, s:s + CK], k))
+            kb.append(cp(q, T.vv[:, lo:lo + n // CK, CK * b:CK * b + CK], T.ps[:, o:o + n], k))
+            ks.append(kb)
         for e in exps:
-            done[e] = [ks[0:2] + k0[0:2], ks[2:4] + k0[2:4]]
-        while nxt[0] in done:
-            e = nxt[0]
+            done[e] = [ks[0:2], ks[2:4]]
+        while nxt in done:
+            e = nxt
             for h in range(2):
                 P = T["pp%d" % h]
                 if e == 0:
                     k_p[(0, h)] = done[0][h]
                 else:
-                    k_p[(e, h)] = run("v", lambda: V.tensor_tensor(P[:, B2 * (e + 1):B2 * (e + 2)], P[:, 0:B2 * (e + 1)].indirect(T.po[:, 6 * e:6 * e + 6]),
-                                                                   T.vv[:, blk(e), B2 * h:B2 * h + B2], A.add), k_p[(e - 1, h)], done[e][h], k_po, c_pp)
-            nxt[0] += 1
+                    k_p[(e, h)] = tt(P[:, B2 * (e + 1):B2 * (e + 2)], P[:, 0:B2 * (e + 1)].indirect(T.po[:, e, :]), T.vv[:, order.index(e), B2 * h:B2 * h + B2],
+                                     A.add, k_p[(e - 1, h)], done[e][h], K["po"], c_pp)
+            nxt += 1
     ny = 0
     for h in range(2):
         ks = []
         for b in (0, 2, 1, 3):
             ks.append(cp("sv"[b // 2], T.yo[:, 512 * h + b:512 * (h + 1):4], T["pp%d" % (b // 2)][:, :].indirect(T.lb[:, 16 * (b % 2) + 8 * h:16 * (b % 2) + 8 * h + 8]),
-                         k_p[(7, b // 2)], k_lb[b % 2]))
+                         k_p[(7, b // 2)], K["lb"]))
         need("y", ks)
         g.sync.dma_start(T.y[:, 512 * h:512 * h + 512], T.yo[:, 512 * h:512 * h + 512]).then_inc(T.sem.dy, 16)
         ny += 16

@@ -3,15 +3,20 @@ from concourse.mybir import dt, AluOpType as A, AxisListType, ActivationFunction
 
 N, TOK, CK = 8, 256, 48
 B4, B2 = 4 * CK, 2 * CK
-NA, NB = 4 * CK, 3 * CK
 PAD = 128 - CK
-OWN = NA + NB + PAD
-SBW = OWN + CK + NA + NB
-RBW = 2 * (NA + NB) + CK
+PIECES = (4, 6, 6)
+NP = N + 1
+OUT1, IN1, SBW = (128, 176, 608, 704), (0, 320, 416, 512), 800
+OUT2, IN2, RBW = (480, 192, 640, 768), (0, 48, 288, 384), 864
+TILES = ((0, 128, 48), (128, 144, 176), (272, 192, 608))
+EXPERT = ((0, 128, 480, 48), (272, 144, 144, 144), (384, 128, 608, 128), (480, 128, 736, 128))
+DECODE = ((0, 192, 1), (256, 128, 2), (352, 128, 3))
+RELU = ("ssss", "ssss", "sssv", "svsv")
+COPY = ("svsv", "svsv", "svss")
 NV, SEG, SH = 9, 258, 16
 ULP = 2.0 ** -24 * (1 + 2.0 ** -6)
 TINY = 2.0 ** -124
-CUT = (10, 0, 5)
+CUT = (2, 2, 1, 0)
 
 SCRATCH = {
     "xs": ("sbuf", [128, 4 * TOK], "bfloat16"),
@@ -32,7 +37,7 @@ SCRATCH = {
     "wgo": ("sbuf", [128, 32], "int32"), "wgu": ("sbuf", [128, 32], "uint16"),
     "col": ("sbuf", [128, 256], "bfloat16"), "val": ("sbuf", [128, TOK], "float32"),
     "meq": ("sbuf", [128, 256], "bfloat16"), "mne": ("sbuf", [128, 256], "bfloat16"),
-    "idw": ("sbuf", [128, 9 * B2], "float32"),
+    "idw": ("sbuf", [128, NP * B2], "float32"),
     "eix": ("sbuf", [128, 128], "float32"), "gm": ("sbuf", [128, 128], "float32"),
     "m1": ("sbuf", [128, 256], "float32"), "fs": ("sbuf", [128, 256], "float32"),
     "ulp": ("sbuf", [128, 256], "float32"), "zz": ("sbuf", [128, 512], "float32"),
@@ -42,12 +47,11 @@ SCRATCH = {
     "rku": ("sbuf", [128, 16], "uint16"),
     "wa": ("sbuf", [128, TOK + SH], "float32"), "wb": ("sbuf", [128, 3, 32], "float32"), "va": ("sbuf", [128, 96], "float32"),
     "oa": ("sbuf", [128, 24], "float32"), "of": ("sbuf", [128, 26], "uint16"),
-    "xt": ("sbuf", [128, 4 * (OWN + CK)], "bfloat16"),
+    "xt": ("sbuf", [128, 4 * (128 + 7 * CK)], "bfloat16"),
     "sb": ("sbuf", [128, SBW], "float8_e4m3fn_x4"), "ss": ("sbuf", [128, SBW], "uint8"),
-    "ht": ("sbuf", [128, 4 * N * CK], "bfloat16"),
+    "ht": ("sbuf", [128, 4, 4 * 3 * CK], "bfloat16"),
     "rb": ("sbuf", [128, RBW], "float8_e4m3fn_x4"), "rs": ("sbuf", [128, RBW], "uint8"),
-    "tk": ("sbuf", [128, 16], "float32"), "pb": ("sbuf", [128, 16], "float32"), "d2": ("sbuf", [128, 32], "float32"),
-    "x1": ("sbuf", [128, 32], "float32"), "yb": ("sbuf", [128, 64], "float32"), "x2": ("sbuf", [128, 2, 32], "float32"),
+    "tk": ("sbuf", [128, 16], "float32"), "pb": ("sbuf", [128, 16], "float32"), "d2": ("sbuf", [128, 16], "float32"),
     "tp": ("sbuf", [128, 2, 128], "float32"),
     "l1": ("sbuf", [128, 2, 64], "float32"), "l2": ("sbuf", [128, 2, 32], "float32"), "l3": ("sbuf", [128, 2, 16], "float32"),
     "k3": ("sbuf", [128, 16], "uint16"), "sel": ("sbuf", [128, 16], "uint16"),
@@ -55,10 +59,10 @@ SCRATCH = {
     "vc": ("sbuf", [128, 96], "float32"), "oc": ("sbuf", [128, 24], "float32"),
     "po": ("sbuf", [128, N, 6], "uint16"), "lb": ("sbuf", [128, 32], "uint16"),
     "vv": ("sbuf", [128, N, B4], "float32"),
-    "pp0": ("sbuf", [128, (N + 1) * B2], "float32"), "pp1": ("sbuf", [128, (N + 1) * B2], "float32"),
+    "pp0": ("sbuf", [128, NP * B2], "float32"), "pp1": ("sbuf", [128, NP * B2], "float32"),
     "yo": ("sbuf", [128, 4 * TOK], "float32"),
 }
-SEMAPHORES = ["v", "s", "t", "p", "dwg", "dx", "dxs", "dw1", "dy", "a1A", "a1B", "a2A", "a2B", "loc"]
+SEMAPHORES = ["v", "s", "t", "p", "dwg", "dx", "dxs", "dw1", "dy", "dt0", "dt1", "loc"] + ["ab"[k] + str(w) for k in range(2) for w in range(4)]
 
 
 def rank_program(g, core, T, topo):
@@ -115,6 +119,9 @@ def rank_program(g, core, T, topo):
 
     FIRST = 4 - (rank & 4)
     STEP = 4 - 2 * FIRST
+    first = [de for de in (1, 2, 3) if topo.mates(core, T.cores[rank ^ de])][0]
+    waves = ((first,), tuple(de for de in (3, 2, 1) if de != first), (7, 6), (5, 4))
+    decoded = [[rank ^ de for de in dels] for dels in (waves[0] + waves[1] + (0,), waves[2], waves[3])]
 
     g.sync.dma_start(T.xs[:, :], T.x[:, :]).then_inc(T.sem.dx, 16)
     g.scalar.dma_start(T.wgs[:, 0:32], T.wg[:, 0:32]).then_inc(T.sem.dwg, 16)
@@ -126,6 +133,7 @@ def rank_program(g, core, T, topo):
     i_pi = run("p", lambda: g.iota(T.pi[:, 0:1], [[0, 1]], 0, 1))
     i_wgo = run("p", lambda: g.iota(T.wgo[:, :], [[4, 4], [4 * STEP, 2], [0, 4]], 4 * FIRST, 0))
     i_col = iota(T.col[:, :], [[0, 16], [1, 16]], 0)
+    i_eix = iota(T.eix[:, :], [[1, 4], [STEP, 2], [0, 16]], 0)
     i_val = iota(T.val[:, :], [[4, TOK]], 0)
     c_msk = run("v", lambda: V.memset(T.msk[:, :], 1.0))
     PI = T.pi[:, 0:1]
@@ -137,8 +145,7 @@ def rank_program(g, core, T, topo):
     for b in range(4):
         s = 2 if b == 1 else 1
         i_em = run("p", lambda: g.affine_select(T.em[:, 512 * b:512 * b + 512], T.msk[:, s:s + 512], [[-1, 512]], A.is_equal, 0.0, b, 4), c_msk)
-    i_eix = iota(T.eix[:, :], [[1, 4], [STEP, 2], [0, 16]], 0)
-    i_idw = iota(T.idw[:, :], [[1, 9 * B2]], 0)
+    i_idw = iota(T.idw[:, :], [[1, NP * B2]], 0)
 
     c_pad = run("v", lambda: V.memset(T.cmv[:, SEG - 1:NV * SEG:SEG], 0.0))
     c_wgu = ts(T.wgu[:, :], T.wgo[:, :], T.bf[:, 0:1], A.add, i_wgo, c_bf)
@@ -154,16 +161,20 @@ def rank_program(g, core, T, topo):
     k_qr = quant(T.qr, T.sr, 0, 128, T.wr[:, :], k_wr)
     k_qx = quant(T.qx, T.sx, 0, TOK, T.xs[:, :], ("dx", 16))
     Z, Z2 = T.ps[:, 3584:3584 + TOK], T.ps[:, 3072:3072 + TOK]
-    k_z2 = run("t", lambda: g.tensor.matmul_mx(Z2, T.qr[:, :], T.sr[:, :], T.qx[:, :], T.sx[:, :], True, True), k_qr, k_qx)
     k_z = run("t", lambda: g.tensor.matmul_mx(Z, T.qr[:, :], T.sr[:, :], T.qx[:, :], T.sx[:, :], True, True), k_qr, k_qx)
-    c_pp = [run("v", lambda: V.memset(T["pp%d" % h][:, 0:B2], 0.0)) for h in range(2)]
-    c_xt = run("v", lambda: V.memset(T.xt[:, 4 * (NA + NB):4 * OWN], 0.0))
+    k_z2 = run("t", lambda: g.tensor.matmul_mx(Z2, T.qr[:, :], T.sr[:, :], T.qx[:, :], T.sx[:, :], True, True), k_qr, k_qx)
+    zero = lambda out, n: run("s", lambda: S.activation(out, T.msk[:, 0:n], F.Copy, scale=0.0), c_msk)
+    c_pp = [zero(T["pp%d" % h][:, 0:B2], B2) for h in range(2)]
+    c_xt = zero(T.xt[:, 0:4 * PAD], 4 * PAD)
+    c_ht = zero(T.ht[:, 0, 4 * CK:512], 4 * PAD)
+    c_gm = ts(T.gm[:, :], T.eix[:, :], T.bp[:, 0:1], A.is_lt, i_eix, c_e)
 
     k_ulp = run("s", lambda: S.activation(T.ulp[:, :], Z2, F.Abs, bias=TINY, scale=ULP), k_z2)
     k_zc = cp("s", T.zz[:, 0:256], Z2, k_z2)
     k_m1 = tt(T.m1[:, :], Z, T.meq[:, :], A.mult, k_z, c_meq)
-    k_zn = tt(T.zz[:, 256:512], Z, T.ulp[:, :], A.add, k_ulp)
     k_fs = run("v", lambda: V.tensor_tensor_scan(T.fs[:, :], T.mne[:, :], T.m1[:, :], 0.0, A.mult, A.add), k_m1, c_mne)
+    k_zn = tt(T.zz[:, 256:512], Z, T.ulp[:, :], A.add, k_ulp)
+    k_eq = tt(T.eq[:, :], Z, T.fs[:, :], A.is_equal, k_fs)
     own = lambda i: T.fs[:, 16 * i + 15:16 * i + 16]
     window = lambda i: T.zz[:, 16 * i + 16:16 * i + 272]
     k_cmp, k_cv, k_ext = [], [], []
@@ -176,49 +187,58 @@ def rank_program(g, core, T, topo):
     for i in range(NV):
         k_cmp.append(ts(T.cmv[:, SEG * i:SEG * i + 256], window(i), own(i), A.is_gt, k_fs, k_zc, k_zn))
         if i == 0:
-            k_eq = tt(T.eq[:, :], Z, T.fs[:, :], A.is_equal)
-        if i == 1:
             k_eqs = run("v", lambda: V.tensor_tensor_scan(T.eqs[:, :], T.mne[:, :], T.eq[:, :], 0.0, A.mult, A.subtract), k_eq)
-        if i == 2:
+        if i == 1:
             k_exs = ts2(T.cms[:, :, 256], T.eqs[:, 16 * NV + 15:256:16], -1.0, A.mult, -float(SH), A.add, k_eqs)
             k_ext.append(cp("v", T.cmv[:, 256:NV * SEG:SEG], T.eqs[:, 15:16 * NV:16]))
         if i == 4:
             count(0)
-            k_last = ts2(T.cms[:, 15 - NV, 0:256], window(15), own(15), A.is_gt, -1.0, A.mult)
     count(1)
     count(2)
     k_sg, k_acc = [], None
     NS = 16 - NV
-    for j in range(NS - 1):
+    for j in range(NS):
         k_sg.append(run("s", lambda: S.activation(T.cms[:, j, 0:256], window(NV + j), F.Sign, bias=own(NV + j), scale=-1.0), k_fs, k_zc, k_zn))
-    k_sg.append(k_last)
     for j in range(NS):
         row = T.cms[:, j, 0:257]
         k_acc = run("s", lambda: S.activation(row, row, F.Relu, scale=-1.0, accum_out=T.acc[:, NV + j:NV + j + 1]), k_sg[j], k_exs)
     k_rku = [cp("v", T.rku[:, NV:16], T.acc[:, NV:16], k_acc), ts(T.rku[:, 0:NV], T.cv[:, 256:NV * SEG:SEG], float(SH), A.add, k_cv)]
 
-    def spread(src, O, w, pk, kc):
+    def spread(src, O, w, pk, kc, qs):
         ks = [[], []]
         for j in range(4):
             for h in range(2):
                 q = 2 * h + j // 2
                 d, o = q ^ (j & 1), w * (q ^ pk)
-                ks[h].append(cp("vs"[h], O(32 * d, 32, o, w), src(q), kc))
+                ks[h].append(cp(qs[h], O(32 * d, 32, o, w), src(q), kc))
             yield
         for h in range(2):
             o = 2 * w * (h ^ (pk >> 1))
-            ks[h].append(cp("vs"[h], O(64 * (1 - h), 64, o, 2 * w), O(64 * h, 64, o, 2 * w), ks[h]))
+            ks[h].append(cp(qs[h], O(64 * (1 - h), 64, o, 2 * w), O(64 * h, 64, o, 2 * w), ks[h]))
         yield ks
 
     k_wa = cp("v", T.wa[:, :].indirect(T.rku[:, 0:16]), T.val[:, :], k_rku, i_val)
+    k = run("s", lambda: S.activation(T.acc[:, 0:NV], T.cv[:, 256:NV * SEG:SEG], F.Identity, bias=float(SH)), k_cv)
+    k_tk = run("s", lambda: S.activation(T.tk[:, :], T.acc[:, :], F.Relu, bias=float(CK + SH), scale=-1.0), k, k_acc)
+    k_pb = run("s", lambda: S.activation(T.pb[:, :], T.acc[:, :], F.Identity, bias=T.bp[:, 2:3]), c_bp)
+    k_tk = run("s", lambda: S.activation(T.tk[:, :], T.tk[:, :], F.Sign), k_tk)
     ks = [cp("vs"[h], T.wb[:, :, 16 * h:16 * h + 16], T.wa[:, SH:SH + CK], k_wa) for h in range(2)]
+    k_d2 = tt(T.d2[:, :], T.tk[:, :], T.pb[:, :], A.mult, k_tk, k_pb)
     k_va = run("v", lambda: V.transpose(T.va[:, :], T.wb[:, :, :]), ks)
-    k_oa = list(spread(lambda q: T.va[32 * q:32 * q + 32, 0:96:16], lambda p, n, o, w: T.oa[p:p + n, o:o + w], 6, (rank & 3) ^ 3, k_va))[-1]
-    k_of = [cp("v", T.of[:, 0:12], T.oa[:, 0:24:2], k_oa), cp("v", T.of[:, 12:21], T.oa[:, 1:18:2])]
+    need("y", k_d2)
+    for j in range(8):
+        g.sync.dma_start(T.tp[0:16, 0, 16 * j:16 * j + 16], T.d2[16 * j:16 * j + 16, :]).then_inc(T.sem.dt0, 16)
+    need("y", ("dt0", 128))
+    for j in range(1, 8):
+        g.sync.dma_start(T.tp[16 * j:16 * j + 16, 0, :], T.tp[0:16, 0, :]).then_inc(T.sem.dt1, 16)
+    k_tp = ("dt1", 112)
+    q0 = (rank ^ first) & 3
+    k_of0 = [cp("v", T.of[32 * d:32 * d + 32, 0:3], T.va[32 * q0:32 * q0 + 32, 16:96:32], k_va) for d in range(4)]
+    k_oa = list(spread(lambda q: T.va[32 * q:32 * q + 32, 0:96:16], lambda p, n, o, w: T.oa[p:p + n, o:o + w], 6, (rank & 3) ^ 3, k_va, "ss"))[-1]
     win = [T.xs[:, :]] + [T["xs%d" % t][:, 16:16 + 4 * TOK - 3] for t in range(1, 4)]
 
-    def gather(a, n, o, k):
-        return [cp("vs"[t // 2], T.xt[:, 4 * a + t:4 * (a + n):4], win[t].indirect(T.of[:, o:o + n // 16]), k, ("dxs", 48) if t else ("dx", 16))
+    def gather(a, n, o, k, qs="vvss"):
+        return [cp(qs[t], T.xt[:, 4 * a + t:4 * (a + n):4], win[t].indirect(T.of[:, o:o + n // 16]), k, ("dxs", 48) if t else ("dx", 16))
                 for t in (2, 0, 3, 1)]
 
     loc = [0]
@@ -226,7 +246,7 @@ def rank_program(g, core, T, topo):
     def send(dels, src_col, dst_col, codes, plane, sem):
         for view in ("q", "s"):
             tr = []
-            per = [2, 2, 2, 2] if len(dels) == 4 else ([4, 2, 2] if view == "q" else [2, 2, 4])
+            per = [8 // len(dels)] * len(dels)
             for j, de in enumerate(dels):
                 dst = T.cores[rank ^ de]
                 eng = topo.engines(core, dst)
@@ -242,39 +262,36 @@ def rank_program(g, core, T, topo):
             g.remote_dma_fused(tr, local_sem=T.sem.loc)
         return (sem, 16)
 
-    FAR, NEAR = (7, 6, 5, 4), (3, 2, 1)
-    need("p", quant(T.sb, T.ss, 0, NA, T.xt[:, 0:4 * NA], gather(0, NA, 0, k_of[0])))
-    arr1 = [send(FAR, 0, OWN + CK, T.sb, T.ss, "a1A")]
-    need("p", quant(T.sb, T.ss, NA, NB, T.xt[:, 4 * NA:4 * (NA + NB)], gather(NA, NB, 12, k_of[1])))
-    arr1.append(send(NEAR, NA, OWN + CK + NA, T.sb, T.ss, "a1B"))
-    k = cp("v", T.of[:, 22:25], T.oa[:, 19:24:2])
+    def tile(j, ks):
+        a, n, b = TILES[j]
+        return quant(T.sb, T.ss, b, n, T.xt[:, 4 * a:4 * (a + n)], ks)
+
+    k_tile = [tile(0, [gather(PAD, CK, 0, k_of0, "vvvv"), c_xt])]
+    o = 6 * (waves[1][0] ^ 3) + 1
+    k_of = [cp("v", T.of[:, 4:10], T.oa[:, o:o + 12:2], k_oa), cp("v", T.of[:, 10:13], T.oa[:, 19:24:2]), cp("v", T.of[:, 14:26], T.oa[:, 0:24:2])]
+    k_tile.append(tile(1, gather(128, 3 * CK, 4, k_of[1])))
+    k_tile.append(tile(2, gather(128 + 3 * CK, 4 * CK, 14, k_of[2])))
+    arr1 = []
+    for w, dels in enumerate(waves):
+        need("p", k_tile[min(w, 2)])
+        arr1.append(send(dels, OUT1[w], IN1[w], T.sb, T.ss, "a%d" % w))
     k_qw = quant(T.qw, T.sw, 0, 512, T.w1s[:, :], ("dw1", 16))
-    k_own = gather(OWN, CK, 22, k)
 
     K = {}
 
+    def decoder(b):
+        K["qe"] = quant(T.qe, T.se, 128 * b, 128, T.em[:, 512 * b:512 * b + 512], i_em)
+
     def combine_lists():
-        k_tk = ts(T.tk[:, :], T.rku[:, :], float(CK + SH), A.is_lt, k_rku)
-        k_pb = ts(T.pb[:, :], T.rku[:, :], T.bp[:, 2:3], A.add, c_bp)
-        K["own"] = quant(T.sb, T.ss, NA + NB, 128, T.xt[:, 4 * (NA + NB):4 * (OWN + CK)], k_own, c_xt)
-        k = [tt(T.d2[:, 16 * h:16 * h + 16], T.tk[:, :], T.pb[:, :], A.mult, k_tk, k_pb) for h in range(2)]
-        k_gm = ts(T.gm[:, :], T.eix[:, :], T.bp[:, 0:1], A.is_lt, i_eix, c_e)
-        yield
-        k = run("v", lambda: V.transpose(T.x1[:, :], T.d2[:, :]), k)
         k_sel = ts(T.sel[:, :], T.va[:, :].indirect(T.selc[:, 0:1]), 0.25, A.mult, c_sel)
+        k = tt(T.tp[:, 1, :], T.tp[:, 0, :], T.gm[:, :], A.mult, k_tp, c_gm)
         yield
-        k = [cp("vs"[h], T.yb[:, 32 * h + 16 * j:32 * h + 16 * j + 16], T.x1[:, 16 * h:16 * h + 16], k) for h in range(2) for j in range(2)]
-        yield
-        k = run("v", lambda: V.transpose(T.x2[:, :, :], T.yb[:, :]), k)
-        yield
-        for k in spread(lambda q: T.x2[32 * q:32 * q + 32, :, 0:16], lambda p, n, o, w: T.tp[p:p + n, 0, o:o + w], 32, 0, k):
-            yield
-        k = tt(T.tp[:, 1, :], T.tp[:, 0, :], T.gm[:, :], A.mult, k, k_gm)
-        yield
-        for a, b, w in ((T.tp, T.l1, 64), (T.l1, T.l2, 32), (T.l2, T.l3, 16)):
+        for j, (a, b, w) in enumerate(((T.tp, T.l1, 64), (T.l1, T.l2, 32), (T.l2, T.l3, 16))):
             k = tt(b[:, :, :], a[:, :, 0:w], a[:, :, w:2 * w], A.max, k)
+            decoder(j)
             yield
         k3 = cp("v", T.k3[:, :], T.l3[:, 1, :], k)
+        decoder(3)
         K["lb"] = [ts(T.lb[:, 16 * b:16 * b + 16], T.l3[:, 0, :], float(CK * b), A.add) for b in range(2)]
         yield
         k = cp("s", T.row[:, :], T.idw[:, :].indirect(T.k3[:, :]), k3, i_idw)
@@ -283,7 +300,7 @@ def rank_program(g, core, T, topo):
         yield
         k = run("v", lambda: V.transpose(T.vc[:, :], T.wd[:, :]), k)
         yield
-        for k in spread(lambda q: T.vc[32 * q:32 * q + 32, 0:96:16], lambda p, n, o, w: T.oc[p:p + n, o:o + w], 6, 0, k):
+        for k in spread(lambda q: T.vc[32 * q:32 * q + 32, 0:96:16], lambda p, n, o, w: T.oc[p:p + n, o:o + w], 6, 0, k, "vs"):
             yield
         K["po"] = [ts(T.po[:, e:e + 4, 3 * b:3 * b + 3], T.oc[:, h:24:2], float(CK * b), A.add, k)
                    for h, e in ((0, FIRST), (1, FIRST + STEP)) for b in range(2)]
@@ -294,52 +311,50 @@ def rank_program(g, core, T, topo):
         for _ in range(n):
             next(steps, None)
 
-    chunk1 = ((OWN, CK + NA), (OWN + CK + NA, NB))
-    chunk2 = ((NA, CK + NA), (2 * NA + CK, NB))
-    free, arr2, k_q2 = {}, [], []
-    for c in range(2):
+    free, arr2, k_q2, nbank = {}, [], [], 0
+    for c, dels in enumerate(waves):
         advance(CUT[c])
-        (a, n), o = chunk1[c], 4 * (CK + NA) * c
+        a, n, o, m = EXPERT[c]
         ks = []
         for i in range(4):
-            src = T.ps[:, 512 * (4 * c + i):512 * (4 * c + i) + n]
-            k = run("t", lambda: g.tensor.matmul_mx(src, T.qw[:, 128 * i:128 * i + 128], T.sw[:, 128 * i:128 * i + 128],
-                                                    T.sb[:, a:a + n], T.ss[:, a:a + n], True, True), arr1[c], k_qw, K["own"], k_rku)
-            out = T.ht[:, o + i:o + 4 * n:4]
-            if i % 2 == 0:
+            bank, nbank = nbank % 8, nbank + 1
+            src = T.ps[:, 512 * bank:512 * bank + n]
+            k = run("t", lambda: g.tensor.matmul_mx(src, T.qw[:, 128 * i:128 * i + 128], T.sw[:, 128 * i:128 * i + 128], T.sb[:, a:a + n], T.ss[:, a:a + n], True, True),
+                    arr1[c], k_qw, k_tile[min(c, 1)], k_rku, free.get(bank))
+            out, src = T.ht[:, c, i:4 * m:4], T.ps[:, 512 * bank:512 * bank + m]
+            if RELU[c][i] == "s":
                 ks.append(run("s", lambda: S.activation(out, src, F.Relu, scale=0.05), k))
             else:
                 ks.append(ts2(out, src, 0.0, A.max, 0.05, A.mult, k))
-            free[4 * c + i] = ks[i]
-        k_q2.append(quant(T.rb, T.rs, chunk2[c][0], n, T.ht[:, o:o + 4 * n], ks))
+            free[bank] = ks[i]
+        k_q2.append(quant(T.rb, T.rs, o, n, T.ht[:, c, 0:4 * n], ks, c_ht))
         need("p", k_q2[c])
-        if c == 0:
-            arr2.append(send(FAR, NA + CK, 0, T.rb, T.rs, "a2A"))
-        else:
-            arr2.append(send(NEAR, 2 * NA + CK, RBW - NB, T.rb, T.rs, "a2B"))
-    advance(CUT[2])
-    k_qe = quant(T.qe, T.se, 0, 512, T.em[:, :], i_em)
+        arr2.append(send(dels, OUT2[c], IN2[c], T.rb, T.rs, "b%d" % c))
     advance(99)
+    k_qe = K["qe"]
 
-    chunk3 = ((0, NA + CK), (RBW - NB, NB))
-    order = [rank ^ de for de in FAR + (0,) + NEAR]
+    order = []
     done, k_p, nxt = {}, {}, 0
-    for c in range(2):
-        a, n = chunk3[c]
-        lo = 5 * c
-        exps = order[lo:lo + n // CK]
+    for c, exps in enumerate(decoded):
+        lo, m = len(order), CK * len(exps)
+        a, n, last = DECODE[c]
+        order += exps
         ks = []
         for b in range(4):
-            o = 512 * (4 * c + b)
+            bank, nbank = nbank % 8, nbank + 1
+            o = 512 * bank
             k = run("t", lambda: g.tensor.matmul_mx(T.ps[:, o:o + n], T.qe[:, 128 * b:128 * b + 128], T.se[:, 128 * b:128 * b + 128],
-                                                    T.rb[:, a:a + n], T.rs[:, a:a + n], True, True), arr2[c], k_qe, free[4 * c + b], k_q2[0])
-            q = "svss"[b]
-            kb = []
+                                                    T.rb[:, a:a + n], T.rs[:, a:a + n], True, True), arr2[:last + 1], k_qe, free[bank], k_q2[1])
+            q = COPY[c][b]
+            o += n - m
+            kb, j0, j1 = [], 0, len(exps)
             if 0 in exps:
                 p, s = B2 + CK * (b % 2), o + CK * exps.index(0)
                 kb.append(cp(q, T["pp%d" % (b // 2)][:, p:p + CK], T.ps[:, s:s + CK], k))
-            kb.append(cp(q, T.vv[:, lo:lo + n // CK, CK * b:CK * b + CK], T.ps[:, o:o + n], k))
+                j0, j1 = j0 + (exps[0] == 0), j1 - (exps[-1] == 0)
+            kb.append(cp(q, T.vv[:, lo + j0:lo + j1, CK * b:CK * b + CK], T.ps[:, o + CK * j0:o + CK * j1], k))
             ks.append(kb)
+            free[bank] = kb
         for e in exps:
             done[e] = [ks[0:2], ks[2:4]]
         while nxt in done:
@@ -352,14 +367,14 @@ def rank_program(g, core, T, topo):
                     k_p[(e, h)] = tt(P[:, B2 * (e + 1):B2 * (e + 2)], P[:, 0:B2 * (e + 1)].indirect(T.po[:, e, :]), T.vv[:, order.index(e), B2 * h:B2 * h + B2],
                                      A.add, k_p[(e - 1, h)], done[e][h], K["po"], c_pp)
             nxt += 1
-    ny = 0
-    for h in range(2):
+    a = 0
+    for n in PIECES:
         ks = []
         for b in (0, 2, 1, 3):
-            ks.append(cp("sv"[b // 2], T.yo[:, 512 * h + b:512 * (h + 1):4], T["pp%d" % (b // 2)][:, :].indirect(T.lb[:, 16 * (b % 2) + 8 * h:16 * (b % 2) + 8 * h + 8]),
+            ks.append(cp("sv"[b // 2], T.yo[:, 64 * a + b:64 * (a + n):4], T["pp%d" % (b // 2)][:, :].indirect(T.lb[:, 16 * (b % 2) + a:16 * (b % 2) + a + n]),
                          k_p[(7, b // 2)], K["lb"]))
         need("y", ks)
-        g.sync.dma_start(T.y[:, 512 * h:512 * h + 512], T.yo[:, 512 * h:512 * h + 512]).then_inc(T.sem.dy, 16)
-        ny += 16
-    need("y", ("dy", ny))
+        g.sync.dma_start(T.y[:, 64 * a:64 * (a + n)], T.yo[:, 64 * a:64 * (a + n)]).then_inc(T.sem.dy, 16)
+        a += n
+    need("y", ("dy", 16 * len(PIECES)))
     need("p", [("v", cnt["v"]), ("s", cnt["s"]), ("t", cnt["t"]), ("p", cnt["p"]), ("loc", loc[0])])

@@ -6,17 +6,21 @@ B4, B2 = 4 * CK, 2 * CK
 PAD = 128 - CK
 PIECES = (4, 6, 6)
 NP = N + 1
-OUT1, IN1, SBW = (128, 176, 608, 704), (0, 320, 416, 512), 800
-OUT2, IN2, RBW = (480, 192, 640, 768), (0, 48, 288, 384), 864
-TILES = ((0, 128, 48), (128, 144, 176), (272, 192, 608))
-EXPERT = ((0, 128, 480, 48), (272, 144, 144, 144), (384, 128, 608, 128), (480, 128, 736, 128))
-DECODE = ((0, 192, 1), (256, 128, 2), (352, 128, 3))
-RELU = ("ssss", "ssss", "sssv", "svsv")
-COPY = ("svsv", "svsv", "svss")
-NV, SEG, SH = 9, 258, 16
+OUT1, IN1, SBW = (128, 208, 336, 560), (0, 432, 656, 880), 976
+OUT2, IN2, RBW = (480, 640, 144, 768), (0, 48, 288, 384), 864
+TILES = ((48, 48), (144, 176), (240, 304), (336, 528), (0, 752))
+EXPERT = ((0, 128, 480, 0, 48, 0), (400, 128, 608, 0, 128, 2), (656, 144, 144, 0, 144, 4), (848, 128, 736, 0, 128, 4))
+DECODE = ((0, 144, 1), (240, 144, 2), (352, 128, 3))
+RELU = ("ssss", "ssvv", "sssv", "ssvv")
+COPY = ("sssv", "svsv", "svss")
+LAST = ((0, 0), (1, 0), (0, 1), (1, 1), (0, 2), (0, 3), (1, 2), (1, 3))
+SEG, SH, LOW = 258, 16, 128
+NS, LATE = 8, 4
+BIG = 4096.0
 ULP = 2.0 ** -24 * (1 + 2.0 ** -6)
 TINY = 2.0 ** -124
-CUT = (2, 2, 1, 0)
+ORDER = ("wa wb near send3 half own mul0 lists whole ea places back0 run mul1 back1 before mul2 back2 mul3 back3 row eb last slots zeros turn spread "
+         "decode0 final decode1 adds decode2 adds")
 
 SCRATCH = {
     "xs": ("sbuf", [128, 4 * TOK], "bfloat16"),
@@ -29,40 +33,38 @@ SCRATCH = {
     "qr": ("sbuf", [128, 128], "float8_e4m3fn_x4"), "sr": ("sbuf", [128, 128], "uint8"),
     "qw": ("sbuf", [128, 512], "float8_e4m3fn_x4"), "sw": ("sbuf", [128, 512], "uint8"),
     "msk": ("sbuf", [128, 3 * SEG], "bfloat16"),
-    "em": ("sbuf", [128, 2048], "bfloat16"),
+    "em": ("sbuf", [128, 2, 516], "bfloat16"),
     "qe": ("sbuf", [128, 512], "float8_e4m3fn_x4"), "se": ("sbuf", [128, 512], "uint8"),
     "ps": ("psum", [128, 4096], "float32"),
     "pi": ("sbuf", [128, 4], "int32"), "bi": ("sbuf", [128, 8], "int32"), "bf": ("sbuf", [128, 8], "float32"),
-    "bp": ("sbuf", [128, 4], "float32"), "selc": ("sbuf", [128, 2], "uint16"),
+    "bp": ("sbuf", [128, 8], "float32"), "selc": ("sbuf", [128, 4], "uint16"),
     "wgo": ("sbuf", [128, 32], "int32"), "wgu": ("sbuf", [128, 32], "uint16"),
-    "col": ("sbuf", [128, 256], "bfloat16"), "val": ("sbuf", [128, TOK], "float32"),
-    "meq": ("sbuf", [128, 256], "bfloat16"), "mne": ("sbuf", [128, 256], "bfloat16"),
+    "col": ("sbuf", [128, 256], "bfloat16"), "val": ("sbuf", [128, TOK], "bfloat16"),
+    "meq": ("sbuf", [128, 128], "bfloat16"), "mne": ("sbuf", [128, 128], "bfloat16"),
     "idw": ("sbuf", [128, NP * B2], "float32"),
-    "eix": ("sbuf", [128, 128], "float32"), "gm": ("sbuf", [128, 128], "float32"),
+    "ro": ("sbuf", [128, 8], "int32"), "rou": ("sbuf", [128, 8], "uint16"), "m8": ("sbuf", [128, 128], "bfloat16"),
     "m1": ("sbuf", [128, 256], "float32"), "fs": ("sbuf", [128, 256], "float32"),
     "ulp": ("sbuf", [128, 256], "float32"), "zz": ("sbuf", [128, 512], "float32"),
     "eq": ("sbuf", [128, 256], "bfloat16"), "eqs": ("sbuf", [128, 256], "bfloat16"),
-    "cmv": ("sbuf", [128, NV * SEG], "bfloat16"), "cv": ("sbuf", [128, NV * SEG], "bfloat16"),
-    "cms": ("sbuf", [128, 16 - NV, 264], "bfloat16"), "acc": ("sbuf", [128, 16], "float32"),
-    "rku": ("sbuf", [128, 16], "uint16"),
-    "wa": ("sbuf", [128, TOK + SH], "float32"), "wb": ("sbuf", [128, 3, 32], "float32"), "va": ("sbuf", [128, 96], "float32"),
-    "oa": ("sbuf", [128, 24], "float32"), "of": ("sbuf", [128, 26], "uint16"),
+    "cm": ("sbuf", [128, 16 * SEG], "bfloat16"), "cv": ("sbuf", [128, (16 - NS) * SEG], "bfloat16"), "acc": ("sbuf", [128, 16], "float32"),
+    "rku": ("sbuf", [128, 16 - LATE], "uint16"), "rkl": ("sbuf", [128, LATE], "uint16"),
+    "wa": ("sbuf", [128, TOK + SH], "bfloat16"), "wb": ("sbuf", [128, 3, 32], "bfloat16"), "va": ("sbuf", [128, 96], "bfloat16"),
+    "oa": ("sbuf", [128, 4, 6], "float32"), "of": ("sbuf", [128, 26], "uint16"),
     "xt": ("sbuf", [128, 4 * (128 + 7 * CK)], "bfloat16"),
     "sb": ("sbuf", [128, SBW], "float8_e4m3fn_x4"), "ss": ("sbuf", [128, SBW], "uint8"),
     "ht": ("sbuf", [128, 4, 4 * 3 * CK], "bfloat16"),
     "rb": ("sbuf", [128, RBW], "float8_e4m3fn_x4"), "rs": ("sbuf", [128, RBW], "uint8"),
     "tk": ("sbuf", [128, 16], "float32"), "pb": ("sbuf", [128, 16], "float32"), "d2": ("sbuf", [128, 16], "float32"),
-    "tp": ("sbuf", [128, 2, 128], "float32"),
-    "l1": ("sbuf", [128, 2, 64], "float32"), "l2": ("sbuf", [128, 2, 32], "float32"), "l3": ("sbuf", [128, 2, 16], "float32"),
+    "tp": ("sbuf", [128, 128], "float32"), "tq": ("sbuf", [128, 128], "float32"), "pm": ("sbuf", [128, 136], "float32"),
     "k3": ("sbuf", [128, 16], "uint16"), "sel": ("sbuf", [128, 16], "uint16"),
     "row": ("sbuf", [128, 256], "float32"), "wd": ("sbuf", [128, 96], "float32"),
-    "vc": ("sbuf", [128, 96], "float32"), "oc": ("sbuf", [128, 24], "float32"),
+    "vc": ("sbuf", [128, 96], "float32"), "oc": ("sbuf", [128, 4, 6], "float32"),
     "po": ("sbuf", [128, N, 6], "uint16"), "lb": ("sbuf", [128, 32], "uint16"),
     "vv": ("sbuf", [128, N, B4], "float32"),
     "pp0": ("sbuf", [128, NP * B2], "float32"), "pp1": ("sbuf", [128, NP * B2], "float32"),
     "yo": ("sbuf", [128, 4 * TOK], "float32"),
 }
-SEMAPHORES = ["v", "s", "t", "p", "dwg", "dx", "dxs", "dw1", "dy", "dt0", "dt1", "loc"] + ["ab"[k] + str(w) for k in range(2) for w in range(4)]
+SEMAPHORES = ["v", "s", "t", "p", "dwg", "dx0", "dx1", "dxs", "dw1", "dy", "dt", "loc"] + ["ab"[k] + str(w) for k in range(2) for w in range(4)]
 
 
 def rank_program(g, core, T, topo):
@@ -111,21 +113,31 @@ def rank_program(g, core, T, topo):
     def tt(out, a, b, op, *deps):
         return run("v", lambda: V.tensor_tensor(out, a, b, op), *deps)
 
+    def scan(out, d0, d1, op1, *deps):
+        return run("v", lambda: V.tensor_tensor_scan(out, d0, d1, 0.0, A.mult, op1), *deps)
+
     def quant(codes, plane, a, n, tile, *deps):
         return run("v", lambda: V.quantize_mx(codes[:, a:a + n], plane[:, a:a + n], tile), *deps)
+
+    def act(out, in_, func, scale, bias, *deps):
+        return run("s", lambda: S.activation(out, in_, func, bias=bias, scale=scale), *deps)
 
     def iota(out, pattern, base):
         return run("p", lambda: g.iota(out, pattern, base, 0, allow_small_or_imprecise_dtypes=True))
 
+    def product(out, wc, wp, i, xc, xp, a, n, *deps):
+        return run("t", lambda: g.tensor.matmul_mx(out, wc[:, 128 * i:128 * i + 128], wp[:, 128 * i:128 * i + 128], xc[:, a:a + n], xp[:, a:a + n], True, True), *deps)
+
     FIRST = 4 - (rank & 4)
     STEP = 4 - 2 * FIRST
-    first = [de for de in (1, 2, 3) if topo.mates(core, T.cores[rank ^ de])][0]
-    waves = ((first,), tuple(de for de in (3, 2, 1) if de != first), (7, 6), (5, 4))
-    decoded = [[rank ^ de for de in dels] for dels in (waves[0] + waves[1] + (0,), waves[2], waves[3])]
+    first = [de for de in (1, 2, 3) if topo.same_plane(core, T.cores[rank ^ de])][0]
+    waves = ((first,), (7, 6), (5, 4), tuple(de for de in (3, 2, 1) if de != first))
+    decoded = [[rank ^ de for de in dels] for dels in (waves[0] + waves[1], (0,) + waves[2], waves[3])]
 
-    g.sync.dma_start(T.xs[:, :], T.x[:, :]).then_inc(T.sem.dx, 16)
+    for h in range(2):
+        g.sync.dma_start(T.xs[:, 512 * h:512 * h + 512], T.x[:, 512 * h:512 * h + 512]).then_inc(T.sem["dx%d" % h], 16)
     g.scalar.dma_start(T.wgs[:, 0:32], T.wg[:, 0:32]).then_inc(T.sem.dwg, 16)
-    g.sync.wait_ge(T.sem.dx, 16)
+    need("y", ("dx1", 16))
     for t in range(1, 4):
         g.sync.dma_start(T["xs%d" % t][:, 16 - t:16 - t + 4 * TOK], T.x[:, :]).then_inc(T.sem.dxs, 16)
     g.sync.dma_start(T.w1s[:, :], T.w1[:, :]).then_inc(T.sem.dw1, 16)
@@ -133,248 +145,259 @@ def rank_program(g, core, T, topo):
     i_pi = run("p", lambda: g.iota(T.pi[:, 0:1], [[0, 1]], 0, 1))
     i_wgo = run("p", lambda: g.iota(T.wgo[:, :], [[4, 4], [4 * STEP, 2], [0, 4]], 4 * FIRST, 0))
     i_col = iota(T.col[:, :], [[0, 16], [1, 16]], 0)
-    i_eix = iota(T.eix[:, :], [[1, 4], [STEP, 2], [0, 16]], 0)
-    i_val = iota(T.val[:, :], [[4, TOK]], 0)
-    c_msk = run("v", lambda: V.memset(T.msk[:, :], 1.0))
-    PI = T.pi[:, 0:1]
-    cb = [ts(T.bi[:, 0:1], PI, 3, A.bitwise_and, i_pi), ts(T.bi[:, 1:2], PI, 15, A.bitwise_and), ts(T.bi[:, 2:3], PI, 5, A.arith_shift_right),
-          ts(T.bi[:, 3:4], PI, 16, A.bitwise_and), ts2(T.bi[:, 4:5], PI, 15, A.bitwise_and, 1, A.arith_shift_right)]
-    c_msk = run("v", lambda: V.memset(T.msk[:, 0:3 * SEG:SEG], 0.0), c_msk)
-    c_bf = cp("v", T.bf[:, 0:5], T.bi[:, 0:5], cb)
-    i_em = None
-    for b in range(4):
-        s = 2 if b == 1 else 1
-        i_em = run("p", lambda: g.affine_select(T.em[:, 512 * b:512 * b + 512], T.msk[:, s:s + 512], [[-1, 512]], A.is_equal, 0.0, b, 4), c_msk)
+    c_msk = iota(T.msk[:, :], [[0, 3 * SEG]], 1)
+    c_msk = run("p", lambda: g.iota(T.msk[:, 0:3 * SEG:SEG], [[0, 3]], 0, 0, allow_small_or_imprecise_dtypes=True), c_msk)
+    i_ro = run("p", lambda: g.iota(T.ro[:, :], [[2, 8]], 0, 0))
+    i_val = iota(T.val[:, :], [[1, TOK]], 0)
+    for j in range(2):
+        i_em = run("p", lambda: g.affine_select(T.em[:, j, :], T.msk[:, 1:517], [[-1, 516]], A.is_equal, 0.0, 2 + j, 4), c_msk)
+    c_xt = iota(T.xt[:, 4 * CK:512], [[0, 4 * PAD]], 0)
     i_idw = iota(T.idw[:, :], [[1, NP * B2]], 0)
-
-    c_pad = run("v", lambda: V.memset(T.cmv[:, SEG - 1:NV * SEG:SEG], 0.0))
+    c_ht = iota(T.ht[:, 0, 4 * CK:512], [[0, 4 * PAD]], 0)
+    PI = T.pi[:, 0:1]
+    AND, SHR = A.bitwise_and, A.arith_shift_right
+    R, H16, EF = T.bf[:, 1:2], T.bf[:, 3:4], T.bp[:, 0:1]
+    c_low = run("v", lambda: V.memset(T.cm[:, (NS + 1) * SEG - 1:16 * SEG:SEG], float(LOW)))
+    c_m8 = run("v", lambda: V.memset(T.m8[:, :], 1.0))
+    cb = [ts(T.bi[:, 0:1], PI, 3, AND, i_pi), ts(T.bi[:, 1:2], PI, 15, AND), ts(T.bi[:, 2:3], PI, 5, SHR)]
+    c_bf = cp("v", T.bf[:, 0:2], T.bi[:, 0:2], cb[1])
+    cb += [ts(T.bi[:, 3:4], PI, 16, AND), ts2(T.bi[:, 4:5], PI, 15, AND, 1, SHR)]
     c_wgu = ts(T.wgu[:, :], T.wgo[:, :], T.bf[:, 0:1], A.add, i_wgo, c_bf)
-    R, H16 = T.bf[:, 1:2], T.bf[:, 3:4]
-    c_e = ts2(T.bp[:, 0:1], H16, STEP / 16, A.mult, T.bf[:, 2:3], A.add)
-    c_sel = ts2(T.bp[:, 1:2], T.bf[:, 4:5], 2.0, A.min, 32.0, A.mult)
-    c_meq = ts(T.meq[:, :], T.col[:, :], R, A.is_equal, i_col)
-    c_mne = ts(T.mne[:, :], T.col[:, :], R, A.not_equal)
-    c_bp = ts2(T.bp[:, 2:3], T.bp[:, 0:1], float(B2), A.mult, float(B2 * (1 + FIRST) - SH), A.add, c_e)
-    c_sel = ts(T.selc[:, 0:1], T.bp[:, 1:2], H16, A.add, c_sel)
+    cb += [ts(T.bi[:, 5:6], PI, 7, AND), ts2(T.bi[:, 6:7], PI, 3, SHR, 1, AND)]
+    c_m8 = [run("v", lambda: V.memset(T.m8[:, 0:128:8], 0.0), c_m8), run("v", lambda: V.memset(T.pm[:, 0:8], 0.0))]
+    c_bf = cp("v", T.bf[:, 2:7], T.bi[:, 2:7], cb)
 
     k_wr = [cp("sv"[h], T.wr[:, 256 * h:256 * h + 256], T.wgs[:, 0:32].indirect(T.wgu[:, 16 * h:16 * h + 16]), ("dwg", 16), c_wgu) for h in range(2)]
-    k_qr = quant(T.qr, T.sr, 0, 128, T.wr[:, :], k_wr)
-    k_qx = quant(T.qx, T.sx, 0, TOK, T.xs[:, :], ("dx", 16))
-    Z, Z2 = T.ps[:, 3584:3584 + TOK], T.ps[:, 3072:3072 + TOK]
-    k_z = run("t", lambda: g.tensor.matmul_mx(Z, T.qr[:, :], T.sr[:, :], T.qx[:, :], T.sx[:, :], True, True), k_qr, k_qx)
-    k_z2 = run("t", lambda: g.tensor.matmul_mx(Z2, T.qr[:, :], T.sr[:, :], T.qx[:, :], T.sx[:, :], True, True), k_qr, k_qx)
-    zero = lambda out, n: run("s", lambda: S.activation(out, T.msk[:, 0:n], F.Copy, scale=0.0), c_msk)
-    c_pp = [zero(T["pp%d" % h][:, 0:B2], B2) for h in range(2)]
-    c_xt = zero(T.xt[:, 0:4 * PAD], 4 * PAD)
-    c_ht = zero(T.ht[:, 0, 4 * CK:512], 4 * PAD)
-    c_gm = ts(T.gm[:, :], T.eix[:, :], T.bp[:, 0:1], A.is_lt, i_eix, c_e)
+    k_qx = [quant(T.qx, T.sx, 0, 128, T.xs[:, 0:512], ("dx0", 16)), quant(T.qr, T.sr, 0, 128, T.wr[:, :], k_wr)]
+    c_meq = ts(T.meq[:, :], T.col[:, 0:128], R, A.is_equal, i_col)
+    k_qx = [k_qx, quant(T.qx, T.sx, 128, 128, T.xs[:, 512:1024], ("dx1", 16))]
+    Z, Z2 = [[T.ps[:, 512 * (b - h):512 * (b - h) + 128] for h in range(2)] for b in (7, 5)]
+    k_z, k_z2 = zip(*[[product(out[h], T.qr, T.sr, 0, T.qx, T.sx, 128 * h, 128, k_qx[h]) for out in (Z, Z2)] for h in range(2)])
+    c_e = act(EF, H16, F.Identity, STEP / 16, T.bf[:, 2:3], c_bf)
+    c_ro = act(T.bp[:, 3:4], T.bf[:, 5:6], F.Identity, 16.0, T.bf[:, 6:7])
+    c_sel = act(T.bp[:, 6:7], T.bf[:, 4:5], F.Relu, -32.0, 64.0)
+    c_bp = act(T.bp[:, 2:3], EF, F.Identity, float(B2), float(B2 * (1 + FIRST) - SH), c_e)
+    c_k3 = [act(T.bp[:, 4:5], R, F.Identity, 8.0, EF), act(T.bp[:, 5:6], EF, F.Sign, 1.0, float(FIRST))]
+    c_sel = act(T.bp[:, 1:2], T.bp[:, 6:7], F.Identity, -1.0, 64.0, c_sel)
 
-    k_ulp = run("s", lambda: S.activation(T.ulp[:, :], Z2, F.Abs, bias=TINY, scale=ULP), k_z2)
-    k_zc = cp("s", T.zz[:, 0:256], Z2, k_z2)
-    k_m1 = tt(T.m1[:, :], Z, T.meq[:, :], A.mult, k_z, c_meq)
-    k_fs = run("v", lambda: V.tensor_tensor_scan(T.fs[:, :], T.mne[:, :], T.m1[:, :], 0.0, A.mult, A.add), k_m1, c_mne)
-    k_zn = tt(T.zz[:, 256:512], Z, T.ulp[:, :], A.add, k_ulp)
-    k_eq = tt(T.eq[:, :], Z, T.fs[:, :], A.is_equal, k_fs)
+    half = lambda t, h, o=0: t[:, o + 128 * h:o + 128 * h + 128]
+    c_mne = act(T.mne[:, :], T.meq[:, :], F.Identity, -1.0, 1.0, c_meq)
+    k_ulp = [act(half(T.ulp, 0), Z2[0], F.Abs, ULP, TINY, k_z2[0])]
+    k_zc = [cp("s", half(T.zz, h), Z2[h], k_z2[h]) for h in range(2)]
+    k_ulp.append(act(half(T.ulp, 1), Z2[1], F.Abs, ULP, TINY))
+    k = tt(half(T.m1, 0), Z[0], T.meq[:, :], A.mult, k_z[0], c_meq)
+    k_fs = [scan(half(T.fs, 0), T.mne[:, :], half(T.m1, 0), A.add, k, c_mne)]
+    k = tt(half(T.m1, 1), Z[1], T.meq[:, :], A.mult, k_z[1])
+    k_zn = [tt(half(T.zz, 0, 256), Z[0], half(T.ulp, 0), A.add, k_ulp[0])]
+    k_fs.append(scan(half(T.fs, 1), T.mne[:, :], half(T.m1, 1), A.add, k))
+    k_zn.append(tt(half(T.zz, 1, 256), Z[1], half(T.ulp, 1), A.add, k_ulp[1]))
+    k_eq = [tt(half(T.eq, h), Z[h], half(T.fs, h), A.is_equal, k_fs[h]) for h in range(2)]
     own = lambda i: T.fs[:, 16 * i + 15:16 * i + 16]
+    row = lambda t, i, n: t[:, SEG * i:SEG * i + n]
     window = lambda i: T.zz[:, 16 * i + 16:16 * i + 272]
-    k_cmp, k_cv, k_ext = [], [], []
+    k_cmp = {}
 
-    def count(c):
-        o = 3 * SEG * c
-        k_cv.append(run("v", lambda: V.tensor_tensor_scan(T.cv[:, o:o + 3 * SEG], T.msk[:, :], T.cmv[:, o:o + 3 * SEG], 0.0, A.mult, A.add),
-                        k_cmp[3 * c + 2], k_ext, c_pad, c_msk))
+    def compare(*cols):
+        for i in cols:
+            k_cmp[i] = ts2(row(T.cm, i, 256), window(i), own(i), A.is_gt, -1.0, A.mult, k_fs, k_zc, k_zn)
 
-    for i in range(NV):
-        k_cmp.append(ts(T.cmv[:, SEG * i:SEG * i + 256], window(i), own(i), A.is_gt, k_fs, k_zc, k_zn))
-        if i == 0:
-            k_eqs = run("v", lambda: V.tensor_tensor_scan(T.eqs[:, :], T.mne[:, :], T.eq[:, :], 0.0, A.mult, A.subtract), k_eq)
-        if i == 1:
-            k_exs = ts2(T.cms[:, :, 256], T.eqs[:, 16 * NV + 15:256:16], -1.0, A.mult, -float(SH), A.add, k_eqs)
-            k_ext.append(cp("v", T.cmv[:, 256:NV * SEG:SEG], T.eqs[:, 15:16 * NV:16]))
-        if i == 4:
-            count(0)
-    count(1)
-    count(2)
-    k_sg, k_acc = [], None
-    NS = 16 - NV
-    for j in range(NS):
-        k_sg.append(run("s", lambda: S.activation(T.cms[:, j, 0:256], window(NV + j), F.Sign, bias=own(NV + j), scale=-1.0), k_fs, k_zc, k_zn))
-    for j in range(NS):
-        row = T.cms[:, j, 0:257]
-        k_acc = run("s", lambda: S.activation(row, row, F.Relu, scale=-1.0, accum_out=T.acc[:, NV + j:NV + j + 1]), k_sg[j], k_exs)
-    k_rku = [cp("v", T.rku[:, NV:16], T.acc[:, NV:16], k_acc), ts(T.rku[:, 0:NV], T.cv[:, 256:NV * SEG:SEG], float(SH), A.add, k_cv)]
+    def count(i, n):
+        return scan(row(T.cv, i - NS, SEG * n), T.msk[:, 0:SEG * n], row(T.cm, i, SEG * n), A.subtract, k_cmp[i + n - 1], k_ext, c_low, c_msk)
 
-    def spread(src, O, w, pk, kc, qs):
+    k_eqs = [scan(half(T.eqs, 0), T.mne[:, :], half(T.eq, 0), A.add, k_eq[0])]
+    compare(8)
+    k_eqs.append(scan(half(T.eqs, 1), T.mne[:, :], half(T.eq, 1), A.add, k_eq[1]))
+    compare(9)
+    k_ext = ts(T.cm[:, 256:16 * SEG:SEG], T.eqs[:, 15:256:16], -float(SH), A.add, k_eqs)
+    compare(10, 11, 12)
+    count(8, 3)
+    compare(13, 14, 15)
+    count(11, 3)
+    k_cv = count(14, 2)
+    counts = T.cv[:, SEG - 1:(16 - NS) * SEG:SEG]
+    turn = list(range(LATE, NS)) + list(range(LATE))
+    k_sg = {i: act(row(T.cm, i, 256), window(i), F.Sign, -1.0, own(i), k_fs[0], k_zc, k_zn[0]) for i in turn}
+    k_acc = {i: run("s", lambda: S.activation(row(T.cm, i, 257), row(T.cm, i, 257), F.Relu, scale=-1.0, accum_out=T.acc[:, i:i + 1]), k_sg[i], k_ext) for i in turn}
+    k_rku = [cp("v", T.rku[:, 0:NS - LATE], T.acc[:, LATE:NS], k_acc[NS - 1]), ts(T.rku[:, NS - LATE:16 - LATE], counts, float(LOW), A.add, k_cv)]
+    c_sel = ts(T.selc[:, 0:1], T.bp[:, 1:2], H16, A.add, c_sel)
+    k_wa = cp("v", T.wa[:, :].indirect(T.rku[:, :]), T.val[:, 16 * LATE:256], k_rku, i_val)
+    k_rku = cp("v", T.rkl[:, :], T.acc[:, 0:LATE], k_acc[LATE - 1])
+    c_k3 = ts2(T.selc[:, 2:3], T.bp[:, 4:5], float(FIRST + 7), A.add, T.bp[:, 5:6], A.mult, c_k3)
+    k_wa = cp("v", T.wa[:, :].indirect(T.rkl[:, :]), T.val[:, 0:16 * LATE], k_rku, k_wa)
+
+    def spread(src, O, pk, kc, qs):
         ks = [[], []]
         for j in range(4):
             for h in range(2):
                 q = 2 * h + j // 2
-                d, o = q ^ (j & 1), w * (q ^ pk)
-                ks[h].append(cp(qs[h], O(32 * d, 32, o, w), src(q), kc))
+                d = q ^ (j & 1)
+                ks[h].append(cp(qs[j][h], O[32 * d:32 * d + 32, q ^ pk, :], src(q), kc))
             yield
         for h in range(2):
-            o = 2 * w * (h ^ (pk >> 1))
-            ks[h].append(cp(qs[h], O(64 * (1 - h), 64, o, 2 * w), O(64 * h, 64, o, 2 * w), ks[h]))
+            o = 2 * (h ^ (pk >> 1))
+            ks[h].append(cp(qs[4][h], O[64 * (1 - h):64 * (1 - h) + 64, o:o + 2, :], O[64 * h:64 * h + 64, o:o + 2, :], ks[h]))
         yield ks
 
-    k_wa = cp("v", T.wa[:, :].indirect(T.rku[:, 0:16]), T.val[:, :], k_rku, i_val)
-    k = run("s", lambda: S.activation(T.acc[:, 0:NV], T.cv[:, 256:NV * SEG:SEG], F.Identity, bias=float(SH)), k_cv)
-    k_tk = run("s", lambda: S.activation(T.tk[:, :], T.acc[:, :], F.Relu, bias=float(CK + SH), scale=-1.0), k, k_acc)
-    k_pb = run("s", lambda: S.activation(T.pb[:, :], T.acc[:, :], F.Identity, bias=T.bp[:, 2:3]), c_bp)
-    k_tk = run("s", lambda: S.activation(T.tk[:, :], T.tk[:, :], F.Sign), k_tk)
+    k = act(T.acc[:, NS:16], counts, F.Identity, 1.0, float(LOW), k_cv)
+    k_tk = act(T.tk[:, :], T.acc[:, :], F.Relu, -BIG, BIG * (CK + SH), k)
+    k_pb = act(T.pb[:, :], T.acc[:, :], F.Identity, 1.0, T.bp[:, 2:3], c_bp)
+    k_d2 = tt(T.d2[:, :], T.tk[:, :], T.pb[:, :], A.min, k_tk, k_pb)
     ks = [cp("vs"[h], T.wb[:, :, 16 * h:16 * h + 16], T.wa[:, SH:SH + CK], k_wa) for h in range(2)]
-    k_d2 = tt(T.d2[:, :], T.tk[:, :], T.pb[:, :], A.mult, k_tk, k_pb)
     k_va = run("v", lambda: V.transpose(T.va[:, :], T.wb[:, :, :]), ks)
+    c_ro = ts(T.rou[:, :], T.ro[:, :], T.bp[:, 3:4], A.add, c_ro, i_ro)
     need("y", k_d2)
-    for j in range(8):
-        g.sync.dma_start(T.tp[0:16, 0, 16 * j:16 * j + 16], T.d2[16 * j:16 * j + 16, :]).then_inc(T.sem.dt0, 16)
-    need("y", ("dt0", 128))
-    for j in range(1, 8):
-        g.sync.dma_start(T.tp[16 * j:16 * j + 16, 0, :], T.tp[0:16, 0, :]).then_inc(T.sem.dt1, 16)
-    k_tp = ("dt1", 112)
+    for j in range(16):
+        e, p = j // 4 + FIRST + STEP * (j // 2 % 2), 16 * (j % 2)
+        g.sync.dma_start(T.tp[p:p + 16, 16 * e:16 * e + 16], T.d2[16 * (j // 2):16 * (j // 2) + 16, :]).then_inc(T.sem.dt, 16)
+
     q0 = (rank ^ first) & 3
-    k_of0 = [cp("v", T.of[32 * d:32 * d + 32, 0:3], T.va[32 * q0:32 * q0 + 32, 16:96:32], k_va) for d in range(4)]
-    k_oa = list(spread(lambda q: T.va[32 * q:32 * q + 32, 0:96:16], lambda p, n, o, w: T.oa[p:p + n, o:o + w], 6, (rank & 3) ^ 3, k_va, "ss"))[-1]
+    k_of0 = [ts(T.of[32 * d:32 * d + 32, 0:3], T.va[32 * q0:32 * q0 + 32, 16:96:32], 4.0, A.mult, k_va) for d in range(4)]
+    pk = (rank & 3) ^ 3
+
+    def pair(x):
+        return [cp("s", T.oa[32 * d:32 * d + 32, y, :], T.va[32 * (y ^ pk):32 * (y ^ pk) + 32, 0:96:16], k_va) for y in (2 * x, 2 * x + 1) for d in (y ^ pk, y ^ pk ^ 1)]
+
+    def offsets(o, y, n, h, *deps):
+        p = 64 * ((y ^ pk) >> 1)
+        return [ts(T.of[64 * d:64 * d + 64, o:o + 3 * n], T.oa[p:p + 64, y:y + n, h:6:2], 4.0, A.mult, *deps) for d in range(2)]
+
+    k_oa = pair(0)
     win = [T.xs[:, :]] + [T["xs%d" % t][:, 16:16 + 4 * TOK - 3] for t in range(1, 4)]
 
     def gather(a, n, o, k, qs="vvss"):
-        return [cp(qs[t], T.xt[:, 4 * a + t:4 * (a + n):4], win[t].indirect(T.of[:, o:o + n // 16]), k, ("dxs", 48) if t else ("dx", 16))
-                for t in (2, 0, 3, 1)]
+        return [cp(qs[t], T.xt[:, 4 * a + t:4 * (a + n):4], win[t].indirect(T.of[:, o:o + n // 16]), k, ("dxs", 48)) for t in (2, 0, 3, 1)]
 
-    loc = [0]
+    def tile(j, ks):
+        a, b = TILES[j]
+        return quant(T.sb, T.ss, b, 128, T.xt[:, 4 * a:4 * a + 512], ks)
 
-    def send(dels, src_col, dst_col, codes, plane, sem):
+    sent = []
+
+    def send(w, src_col, dst_col, codes, plane, sem, k):
+        need("p", k)
         for view in ("q", "s"):
             tr = []
-            per = [8 // len(dels)] * len(dels)
-            for j, de in enumerate(dels):
+            for j, de in enumerate(waves[w]):
                 dst = T.cores[rank ^ de]
                 eng = topo.engines(core, dst)
-                mask = sum(1 << e for e in eng[sum(per[:j]):sum(per[:j + 1])])
+                per = len(eng) // len(waves[w])
                 rid, pid = topo.addr(dst, core)
-                a, b = src_col + CK * j, dst_col + CK * j
+                a, b = src_col[w] + CK * j, dst_col[w] + CK * j
                 if view == "q":
                     sa, da = codes[:, a:a + CK].bitcast(dt.uint8), codes[:, b:b + CK].bitcast(dt.uint8)
                 else:
                     sa, da = plane[:, a:a + CK], plane[:, b:b + CK]
-                tr.append(RemoteDMATransfer(dst_ids=[DstId(rid=rid, pnc=pid)], dma_engine_mask=mask, remote_sem=T.sem[sem], src=sa, dst=da))
-                loc[0] += per[j]
+                tr.append(RemoteDMATransfer(dst_ids=[DstId(rid=rid, pnc=pid)], dma_engine_mask=sum(1 << e for e in eng[per * j:per * j + per]),
+                                            remote_sem=T.sem[sem + str(w)], src=sa, dst=da))
             g.remote_dma_fused(tr, local_sem=T.sem.loc)
-        return (sem, 16)
+            sent.append(len(eng))
+        return k
 
-    def tile(j, ks):
-        a, n, b = TILES[j]
-        return quant(T.sb, T.ss, b, n, T.xt[:, 4 * a:4 * (a + n)], ks)
+    k = gather(128, CK, 0, k_of0)
+    k_of = offsets(4, 0, 2, 0, k_oa)
+    k_oa = pair(1)
+    K = {"tile0": tile(0, [k, c_xt])}
+    k = gather(176, 2 * CK, 4, k_of)
+    k_of = offsets(10, 2, 2, 0, k_oa)
+    k_near = [offsets(16, waves[3][0] ^ 3, 1, 1)]
+    K["tile1"] = tile(1, k)
+    k_near.append(offsets(19, waves[3][1] ^ 3, 1, 1))
+    k = gather(272, 2 * CK, 10, k_of)
+    k_own = offsets(22, 3, 1, 1)
+    K["tile2"] = tile(2, k)
+    for w in range(3):
+        send(w, OUT1, IN1, T.sb, T.ss, "a", K["tile%d" % w])
+    WAVE = sent[0] + sent[1]
 
-    k_tile = [tile(0, [gather(PAD, CK, 0, k_of0, "vvvv"), c_xt])]
-    o = 6 * (waves[1][0] ^ 3) + 1
-    k_of = [cp("v", T.of[:, 4:10], T.oa[:, o:o + 12:2], k_oa), cp("v", T.of[:, 10:13], T.oa[:, 19:24:2]), cp("v", T.of[:, 14:26], T.oa[:, 0:24:2])]
-    k_tile.append(tile(1, gather(128, 3 * CK, 4, k_of[1])))
-    k_tile.append(tile(2, gather(128 + 3 * CK, 4 * CK, 14, k_of[2])))
-    arr1 = []
-    for w, dels in enumerate(waves):
-        need("p", k_tile[min(w, 2)])
-        arr1.append(send(dels, OUT1[w], IN1[w], T.sb, T.ss, "a%d" % w))
-    k_qw = quant(T.qw, T.sw, 0, 512, T.w1s[:, :], ("dw1", 16))
+    free, done, k_p = {}, {}, {}
+    order = [e for exps in decoded for e in exps]
 
-    K = {}
-
-    def decoder(b):
-        K["qe"] = quant(T.qe, T.se, 128 * b, 128, T.em[:, 512 * b:512 * b + 512], i_em)
-
-    def combine_lists():
-        k_sel = ts(T.sel[:, :], T.va[:, :].indirect(T.selc[:, 0:1]), 0.25, A.mult, c_sel)
-        k = tt(T.tp[:, 1, :], T.tp[:, 0, :], T.gm[:, :], A.mult, k_tp, c_gm)
-        yield
-        for j, (a, b, w) in enumerate(((T.tp, T.l1, 64), (T.l1, T.l2, 32), (T.l2, T.l3, 16))):
-            k = tt(b[:, :, :], a[:, :, 0:w], a[:, :, w:2 * w], A.max, k)
-            decoder(j)
-            yield
-        k3 = cp("v", T.k3[:, :], T.l3[:, 1, :], k)
-        decoder(3)
-        K["lb"] = [ts(T.lb[:, 16 * b:16 * b + 16], T.l3[:, 0, :], float(CK * b), A.add) for b in range(2)]
-        yield
-        k = cp("s", T.row[:, :], T.idw[:, :].indirect(T.k3[:, :]), k3, i_idw)
-        yield
-        k = cp("s", T.wd[:, :], T.row[:, :].indirect(T.sel[:, 0:6]), k, k_sel)
-        yield
-        k = run("v", lambda: V.transpose(T.vc[:, :], T.wd[:, :]), k)
-        yield
-        for k in spread(lambda q: T.vc[32 * q:32 * q + 32, 0:96:16], lambda p, n, o, w: T.oc[p:p + n, o:o + w], 6, 0, k, "vs"):
-            yield
-        K["po"] = [ts(T.po[:, e:e + 4, 3 * b:3 * b + 3], T.oc[:, h:24:2], float(CK * b), A.add, k)
-                   for h, e in ((0, FIRST), (1, FIRST + STEP)) for b in range(2)]
-
-    steps = combine_lists()
-
-    def advance(n):
-        for _ in range(n):
-            next(steps, None)
-
-    free, arr2, k_q2, nbank = {}, [], [], 0
-    for c, dels in enumerate(waves):
-        advance(CUT[c])
-        a, n, o, m = EXPERT[c]
+    def mul(c):
+        a, n, o, lo, hi, j = EXPERT[c]
         ks = []
         for i in range(4):
-            bank, nbank = nbank % 8, nbank + 1
-            src = T.ps[:, 512 * bank:512 * bank + n]
-            k = run("t", lambda: g.tensor.matmul_mx(src, T.qw[:, 128 * i:128 * i + 128], T.sw[:, 128 * i:128 * i + 128], T.sb[:, a:a + n], T.ss[:, a:a + n], True, True),
-                    arr1[c], k_qw, k_tile[min(c, 1)], k_rku, free.get(bank))
-            out, src = T.ht[:, c, i:4 * m:4], T.ps[:, 512 * bank:512 * bank + m]
-            if RELU[c][i] == "s":
-                ks.append(run("s", lambda: S.activation(out, src, F.Relu, scale=0.05), k))
-            else:
-                ks.append(ts2(out, src, 0.0, A.max, 0.05, A.mult, k))
+            bank = (4 * c + i) % 8
+            k = product(T.ps[:, 512 * bank:512 * bank + n], T.qw, T.sw, i, T.sb, T.ss, a, n, ("a%d" % c, WAVE), K["wa" if i < 2 else "wb"], K["tile%d" % j], k_rku, free.get(bank))
+            out, src = T.ht[:, c, 4 * lo + i:4 * hi:4], T.ps[:, 512 * bank + lo:512 * bank + hi]
+            ks.append(act(out, src, F.Relu, 0.05, 0.0, k) if RELU[c][i] == "s" else ts2(out, src, 0.0, A.max, 0.05, A.mult, k))
             free[bank] = ks[i]
-        k_q2.append(quant(T.rb, T.rs, o, n, T.ht[:, c, 0:4 * n], ks, c_ht))
-        need("p", k_q2[c])
-        arr2.append(send(dels, OUT2[c], IN2[c], T.rb, T.rs, "b%d" % c))
-    advance(99)
-    k_qe = K["qe"]
+        return ks
 
-    order = []
-    done, k_p, nxt = {}, {}, 0
-    for c, exps in enumerate(decoded):
-        lo, m = len(order), CK * len(exps)
+    def back(c):
+        a, n, o, lo, hi, j = EXPERT[c]
+        return send(c, OUT2, IN2, T.rb, T.rs, "b", quant(T.rb, T.rs, o, n, T.ht[:, c, 0:4 * n], K["mul%d" % c], c_ht))
+
+    def decode(c):
+        exps = decoded[c]
+        lo, m = order.index(exps[0]), CK * len(exps)
         a, n, last = DECODE[c]
-        order += exps
-        ks = []
-        for b in range(4):
-            bank, nbank = nbank % 8, nbank + 1
-            o = 512 * bank
-            k = run("t", lambda: g.tensor.matmul_mx(T.ps[:, o:o + n], T.qe[:, 128 * b:128 * b + 128], T.se[:, 128 * b:128 * b + 128],
-                                                    T.rb[:, a:a + n], T.rs[:, a:a + n], True, True), arr2[:last + 1], k_qe, free[bank], k_q2[1])
-            q = COPY[c][b]
-            o += n - m
-            kb, j0, j1 = [], 0, len(exps)
-            if 0 in exps:
-                p, s = B2 + CK * (b % 2), o + CK * exps.index(0)
-                kb.append(cp(q, T["pp%d" % (b // 2)][:, p:p + CK], T.ps[:, s:s + CK], k))
-                j0, j1 = j0 + (exps[0] == 0), j1 - (exps[-1] == 0)
-            kb.append(cp(q, T.vv[:, lo + j0:lo + j1, CK * b:CK * b + CK], T.ps[:, o + CK * j0:o + CK * j1], k))
-            ks.append(kb)
-            free[bank] = kb
-        for e in exps:
-            done[e] = [ks[0:2], ks[2:4]]
-        while nxt in done:
-            e = nxt
+        banks = [(4 * c + b) % 8 for b in range(4)]
+        k_d = [product(T.ps[:, 512 * banks[b]:512 * banks[b] + n], T.qe, T.se, b, T.rb, T.rs, a, n,
+                       [("b%d" % w, WAVE) for w in range(last + 1)], K["ea"], K["eb"], free[banks[b]], K["back2"] if c else None) for b in range(4)]
+        runs = [(j, j + 1) for j in sorted(range(2), key=lambda j: exps[j])] if c == 2 else [(0, len(exps))]
+        if c < 2 and 0 in exps:
+            j = exps.index(0)
+            runs = [(j, j + 1), (int(j == 0), len(exps) - (j == len(exps) - 1))]
+        ks = {}
+        for x, b in LAST if c == 2 else [(x, b) for x in range(len(runs)) for b in range(4)]:
+            (j0, j1), o = runs[x], 512 * banks[b] + n - m
+            if exps[j0:j1] == [0]:
+                out = T["pp%d" % (b // 2)][:, B2 + CK * (b % 2):B2 + CK * (b % 2) + CK]
+            else:
+                out = T.vv[:, lo + j0:lo + j1, CK * b:CK * b + CK]
+            ks[x, b] = free[banks[b]] = cp(COPY[c][b], out, T.ps[:, o + CK * j0:o + CK * j1], k_d[b])
+        for x, (j0, j1) in enumerate(runs):
+            for e in exps[j0:j1]:
+                done.setdefault(e, [[ks[x, 0], ks[x, 1]], [ks[x, 2], ks[x, 3]]])
+
+    def adds():
+        for e in range(len(k_p) // 2, N):
+            if e not in done:
+                break
             for h in range(2):
                 P = T["pp%d" % h]
-                if e == 0:
-                    k_p[(0, h)] = done[0][h]
-                else:
-                    k_p[(e, h)] = tt(P[:, B2 * (e + 1):B2 * (e + 2)], P[:, 0:B2 * (e + 1)].indirect(T.po[:, e, :]), T.vv[:, order.index(e), B2 * h:B2 * h + B2],
-                                     A.add, k_p[(e - 1, h)], done[e][h], K["po"], c_pp)
-            nxt += 1
+                k_p[(e, h)] = done[0][h] if e == 0 else tt(
+                    P[:, B2 * (e + 1):B2 * (e + 2)], P[:, 0:B2 * (e + 1)].indirect(T.po[:, e, :]), T.vv[:, order.index(e), B2 * h:B2 * h + B2],
+                    A.add, k_p[(e - 1, h)], done[e][h], K["final"], K["zeros"])
+
+    def own_lists():
+        K["tile4"] = tile(4, K["own"])
+        return cp("v", T.sel[:, :], T.va[:, :].indirect(T.selc[:, 0:1]), c_sel)
+
+    step = {
+        "near": lambda: gather(368, 2 * CK, 16, k_near, "ssss"),
+        "own": lambda: gather(0, CK, 22, k_own, "ssss"),
+        "zeros": lambda: [run("s", lambda: S.activation(P[:, 0:B2], T.col[:, 0:B2], F.Copy, scale=0.0), i_col) for P in (T.pp0, T.pp1)],
+        "wa": lambda: quant(T.qw, T.sw, 0, 256, T.w1s[:, 0:1024], ("dw1", 16)),
+        "wb": lambda: quant(T.qw, T.sw, 256, 256, T.w1s[:, 1024:2048]),
+        "ea": lambda: [quant(T.qe, T.se, 128 * b, 128, T.em[:, b, 2:514], i_em) for b in range(2)],
+        "eb": lambda: [quant(T.qe, T.se, 256 + 128 * b, 128, T.em[:, b, 0:512], i_em) for b in range(2)],
+        "send3": lambda: send(3, OUT1, IN1, T.sb, T.ss, "a", tile(3, K["near"])),
+        "lists": own_lists, "adds": adds,
+        "half": lambda: cp("v", T.tp[32:64, :], T.tp[0:32, :], ("dt", 256)),
+        "whole": lambda: cp("v", T.tp[64:128, :], T.tp[0:64, :], K["half"]),
+        "places": lambda: cp("s", T.tq[:, :], T.tp[:, :].indirect(T.rou[:, :]), c_ro, K["whole"]),
+        "run": lambda: scan(T.pm[:, 8:136], T.m8[:, :], T.tq[:, :], A.max, K["places"], c_m8),
+        "before": lambda: cp("v", T.k3[:, :], T.pm[:, :].indirect(T.selc[:, 2:3]), K["run"], c_k3),
+        "last": lambda: [ts(T.lb[:, 16 * b:16 * b + 16], T.pm[:, 15:136:8], float(CK * b), A.add, K["run"]) for b in range(2)],
+        "row": lambda: cp("s", T.row[:, :], T.idw[:, :].indirect(T.k3[:, :]), K["before"], i_idw),
+        "slots": lambda: cp("s", T.wd[:, :], T.row[:, :].indirect(T.sel[:, 0:6]), K["row"], K["lists"]),
+        "turn": lambda: run("v", lambda: V.transpose(T.vc[:, :], T.wd[:, :]), K["slots"]),
+        "spread": lambda: list(spread(lambda q: T.vc[32 * q:32 * q + 32, 0:96:16], T.oc, 0, K["turn"], ("vv",) * 5))[-1],
+        "final": lambda: [ts(T.po[:, e:e + 4, 3 * b:3 * b + 3], T.oc[:, :, h:6:2], float(CK * b), A.add, K["spread"])
+                          for h, e in ((0, FIRST), (1, FIRST + STEP)) for b in range(2)],
+    }
+    for name in ORDER.split():
+        K[name] = step[name]() if name in step else {"mul": mul, "back": back, "decode": decode}[name[:-1]](int(name[-1]))
+
     a = 0
     for n in PIECES:
         ks = []
-        for b in (0, 2, 1, 3):
-            ks.append(cp("sv"[b // 2], T.yo[:, 64 * a + b:64 * (a + n):4], T["pp%d" % (b // 2)][:, :].indirect(T.lb[:, 16 * (b % 2) + a:16 * (b % 2) + a + n]),
-                         k_p[(7, b // 2)], K["lb"]))
+        for b in range(4):
+            ks.append(cp("sv"[b % 2], T.yo[:, 64 * a + b:64 * (a + n):4], T["pp%d" % (b // 2)][:, :].indirect(T.lb[:, 16 * (b % 2) + a:16 * (b % 2) + a + n]),
+                         k_p[(7, b // 2)], K["last"]))
         need("y", ks)
         g.sync.dma_start(T.y[:, 64 * a:64 * (a + n)], T.yo[:, 64 * a:64 * (a + n)]).then_inc(T.sem.dy, 16)
         a += n
     need("y", ("dy", 16 * len(PIECES)))
-    need("p", [("v", cnt["v"]), ("s", cnt["s"]), ("t", cnt["t"]), ("p", cnt["p"]), ("loc", loc[0])])
+    need("p", [("v", cnt["v"]), ("s", cnt["s"]), ("t", cnt["t"]), ("p", cnt["p"]), ("loc", sum(sent))])

from concourse.bass import DstId, RemoteDMATransfer
from concourse.mybir import dt, AluOpType as A, AxisListType, ActivationFunctionType as F

N, TOK, CK = 8, 256, 48
B4, B2 = 4 * CK, 2 * CK
PAD = 128 - CK
PIECES = (4, 6, 6)
NP = N + 1
OUT1, IN1, SBW = (128, 208, 336, 560), (0, 432, 656, 880), 976
OUT2, IN2, RBW = (480, 640, 144, 768), (0, 48, 288, 384), 864
TILES = ((48, 48), (144, 176), (240, 304), (336, 528), (0, 752))
EXPERT = ((0, 128, 480, 0, 48, 0), (400, 128, 608, 0, 128, 2), (656, 144, 144, 0, 144, 4), (848, 128, 736, 0, 128, 4))
DECODE = ((0, 144, 1), (240, 144, 2), (352, 128, 3))
RELU = ("ssss", "ssvv", "sssv", "ssvv")
COPY = ("sssv", "svsv", "svss")
LAST = ((0, 0), (1, 0), (0, 1), (1, 1), (0, 2), (0, 3), (1, 2), (1, 3))
SEG, SH, LOW = 258, 16, 128
NS, LATE = 8, 4
BIG = 4096.0
ULP = 2.0 ** -24 * (1 + 2.0 ** -6)
TINY = 2.0 ** -124
ORDER = ("wa wb near send3 half own mul0 lists whole ea places back0 run mul1 back1 before mul2 back2 mul3 back3 row eb last slots zeros turn spread "
         "decode0 final decode1 adds decode2 adds")

SCRATCH = {
    "xs": ("sbuf", [128, 4 * TOK], "bfloat16"),
    "xs1": ("sbuf", [128, 4 * TOK + 16], "bfloat16"), "xs2": ("sbuf", [128, 4 * TOK + 16], "bfloat16"),
    "xs3": ("sbuf", [128, 4 * TOK + 16], "bfloat16"),
    "wgs": ("sbuf", [128, 32], "bfloat16"),
    "wr": ("sbuf", [128, 512], "bfloat16"),
    "w1s": ("sbuf", [128, 2048], "bfloat16"),
    "qx": ("sbuf", [128, TOK], "float8_e4m3fn_x4"), "sx": ("sbuf", [128, TOK], "uint8"),
    "qr": ("sbuf", [128, 128], "float8_e4m3fn_x4"), "sr": ("sbuf", [128, 128], "uint8"),
    "qw": ("sbuf", [128, 512], "float8_e4m3fn_x4"), "sw": ("sbuf", [128, 512], "uint8"),
    "msk": ("sbuf", [128, 3 * SEG], "bfloat16"),
    "em": ("sbuf", [128, 2, 516], "bfloat16"),
    "qe": ("sbuf", [128, 512], "float8_e4m3fn_x4"), "se": ("sbuf", [128, 512], "uint8"),
    "ps": ("psum", [128, 4096], "float32"),
    "pi": ("sbuf", [128, 4], "int32"), "bi": ("sbuf", [128, 8], "int32"), "bf": ("sbuf", [128, 8], "float32"),
    "bp": ("sbuf", [128, 8], "float32"), "selc": ("sbuf", [128, 4], "uint16"),
    "wgo": ("sbuf", [128, 32], "int32"), "wgu": ("sbuf", [128, 32], "uint16"),
    "col": ("sbuf", [128, 256], "bfloat16"), "val": ("sbuf", [128, TOK], "bfloat16"),
    "meq": ("sbuf", [128, 128], "bfloat16"), "mne": ("sbuf", [128, 128], "bfloat16"),
    "idw": ("sbuf", [128, NP * B2], "float32"),
    "ro": ("sbuf", [128, 8], "int32"), "rou": ("sbuf", [128, 8], "uint16"), "m8": ("sbuf", [128, 128], "bfloat16"),
    "m1": ("sbuf", [128, 256], "float32"), "fs": ("sbuf", [128, 256], "float32"),
    "ulp": ("sbuf", [128, 256], "float32"), "zz": ("sbuf", [128, 512], "float32"),
    "eq": ("sbuf", [128, 256], "bfloat16"), "eqs": ("sbuf", [128, 256], "bfloat16"),
    "cm": ("sbuf", [128, 16 * SEG], "bfloat16"), "cv": ("sbuf", [128, (16 - NS) * SEG], "bfloat16"), "acc": ("sbuf", [128, 16], "float32"),
    "rku": ("sbuf", [128, 16 - LATE], "uint16"), "rkl": ("sbuf", [128, LATE], "uint16"),
    "wa": ("sbuf", [128, TOK + SH], "bfloat16"), "wb": ("sbuf", [128, 3, 32], "bfloat16"), "va": ("sbuf", [128, 96], "bfloat16"),
    "oa": ("sbuf", [128, 4, 6], "float32"), "of": ("sbuf", [128, 26], "uint16"),
    "xt": ("sbuf", [128, 4 * (128 + 7 * CK)], "bfloat16"),
    "sb": ("sbuf", [128, SBW], "float8_e4m3fn_x4"), "ss": ("sbuf", [128, SBW], "uint8"),
    "ht": ("sbuf", [128, 4, 4 * 3 * CK], "bfloat16"),
    "rb": ("sbuf", [128, RBW], "float8_e4m3fn_x4"), "rs": ("sbuf", [128, RBW], "uint8"),
    "tk": ("sbuf", [128, 16], "float32"), "pb": ("sbuf", [128, 16], "float32"), "d2": ("sbuf", [128, 16], "float32"),
    "tp": ("sbuf", [128, 128], "float32"), "tq": ("sbuf", [128, 128], "float32"), "pm": ("sbuf", [128, 136], "float32"),
    "k3": ("sbuf", [128, 16], "uint16"), "sel": ("sbuf", [128, 16], "uint16"),
    "row": ("sbuf", [128, 256], "float32"), "wd": ("sbuf", [128, 96], "float32"),
    "vc": ("sbuf", [128, 96], "float32"), "oc": ("sbuf", [128, 4, 6], "float32"),
    "po": ("sbuf", [128, N, 6], "uint16"), "lb": ("sbuf", [128, 32], "uint16"),
    "vv": ("sbuf", [128, N, B4], "float32"),
    "pp0": ("sbuf", [128, NP * B2], "float32"), "pp1": ("sbuf", [128, NP * B2], "float32"),
    "yo": ("sbuf", [128, 4 * TOK], "float32"),
}
SEMAPHORES = ["v", "s", "t", "p", "dwg", "dx0", "dx1", "dxs", "dw1", "dy", "dt", "loc"] + ["ab"[k] + str(w) for k in range(2) for w in range(4)]


def rank_program(g, core, T, topo):
    rank = T.rank_of(core)
    if rank is None:
        return
    Q = {"v": g.vector, "s": g.scalar, "t": g.tensor, "p": g, "y": g.sync}
    cnt = {"v": 0, "s": 0, "t": 0, "p": 0}
    known = {}

    def flat(deps):
        for d in deps:
            if isinstance(d, list):
                yield from flat(d)
            elif d is not None:
                yield d

    def need(q, *deps):
        best = {}
        for sem, val in flat(deps):
            best[sem] = max(best.get(sem, 0), val)
        for sem, val in best.items():
            if known.get((q, sem), 0) < val:
                Q[q].wait_ge(T.sem[sem], val)
                known[(q, sem)] = val

    def run(q, fn, *deps):
        need(q, *deps)
        cnt[q] += 1
        fn().then_inc(T.sem[q], 1)
        return (q, cnt[q])

    V, S = g.vector, g.scalar

    def cp(q, out, in_, *deps):
        if q == "v":
            return run("v", lambda: V.tensor_copy(out, in_), *deps)
        return run("s", lambda: S.activation(out, in_, F.Copy), *deps)

    def ts(out, in0, s1, op0, *deps):
        return run("v", lambda: V.tensor_scalar(out, in0, s1, None, op0), *deps)

    def ts2(out, in0, s1, op0, s2, op1, *deps):
        return run("v", lambda: V.tensor_scalar(out, in0, s1, s2, op0, op1), *deps)

    def tt(out, a, b, op, *deps):
        return run("v", lambda: V.tensor_tensor(out, a, b, op), *deps)

    def scan(out, d0, d1, op1, *deps):
        return run("v", lambda: V.tensor_tensor_scan(out, d0, d1, 0.0, A.mult, op1), *deps)

    def quant(codes, plane, a, n, tile, *deps):
        return run("v", lambda: V.quantize_mx(codes[:, a:a + n], plane[:, a:a + n], tile), *deps)

    def act(out, in_, func, scale, bias, *deps):
        return run("s", lambda: S.activation(out, in_, func, bias=bias, scale=scale), *deps)

    def iota(out, pattern, base):
        return run("p", lambda: g.iota(out, pattern, base, 0, allow_small_or_imprecise_dtypes=True))

    def product(out, wc, wp, i, xc, xp, a, n, *deps):
        return run("t", lambda: g.tensor.matmul_mx(out, wc[:, 128 * i:128 * i + 128], wp[:, 128 * i:128 * i + 128], xc[:, a:a + n], xp[:, a:a + n], True, True), *deps)

    FIRST = 4 - (rank & 4)
    STEP = 4 - 2 * FIRST
    first = [de for de in (1, 2, 3) if topo.same_plane(core, T.cores[rank ^ de])][0]
    waves = ((first,), (7, 6), (5, 4), tuple(de for de in (3, 2, 1) if de != first))
    decoded = [[rank ^ de for de in dels] for dels in (waves[0] + waves[1], (0,) + waves[2], waves[3])]

    for h in range(2):
        g.sync.dma_start(T.xs[:, 512 * h:512 * h + 512], T.x[:, 512 * h:512 * h + 512]).then_inc(T.sem["dx%d" % h], 16)
    g.scalar.dma_start(T.wgs[:, 0:32], T.wg[:, 0:32]).then_inc(T.sem.dwg, 16)
    need("y", ("dx1", 16))
    for t in range(1, 4):
        g.sync.dma_start(T["xs%d" % t][:, 16 - t:16 - t + 4 * TOK], T.x[:, :]).then_inc(T.sem.dxs, 16)
    g.sync.dma_start(T.w1s[:, :], T.w1[:, :]).then_inc(T.sem.dw1, 16)

    i_pi = run("p", lambda: g.iota(T.pi[:, 0:1], [[0, 1]], 0, 1))
    i_wgo = run("p", lambda: g.iota(T.wgo[:, :], [[4, 4], [4 * STEP, 2], [0, 4]], 4 * FIRST, 0))
    i_col = iota(T.col[:, :], [[0, 16], [1, 16]], 0)
    c_msk = iota(T.msk[:, :], [[0, 3 * SEG]], 1)
    c_msk = run("p", lambda: g.iota(T.msk[:, 0:3 * SEG:SEG], [[0, 3]], 0, 0, allow_small_or_imprecise_dtypes=True), c_msk)
    i_ro = run("p", lambda: g.iota(T.ro[:, :], [[2, 8]], 0, 0))
    i_val = iota(T.val[:, :], [[1, TOK]], 0)
    for j in range(2):
        i_em = run("p", lambda: g.affine_select(T.em[:, j, :], T.msk[:, 1:517], [[-1, 516]], A.is_equal, 0.0, 2 + j, 4), c_msk)
    c_xt = iota(T.xt[:, 4 * CK:512], [[0, 4 * PAD]], 0)
    i_idw = iota(T.idw[:, :], [[1, NP * B2]], 0)
    c_ht = iota(T.ht[:, 0, 4 * CK:512], [[0, 4 * PAD]], 0)
    PI = T.pi[:, 0:1]
    AND, SHR = A.bitwise_and, A.arith_shift_right
    R, H16, EF = T.bf[:, 1:2], T.bf[:, 3:4], T.bp[:, 0:1]
    c_low = run("v", lambda: V.memset(T.cm[:, (NS + 1) * SEG - 1:16 * SEG:SEG], float(LOW)))
    c_m8 = run("v", lambda: V.memset(T.m8[:, :], 1.0))
    cb = [ts(T.bi[:, 0:1], PI, 3, AND, i_pi), ts(T.bi[:, 1:2], PI, 15, AND), ts(T.bi[:, 2:3], PI, 5, SHR)]
    c_bf = cp("v", T.bf[:, 0:2], T.bi[:, 0:2], cb[1])
    cb += [ts(T.bi[:, 3:4], PI, 16, AND), ts2(T.bi[:, 4:5], PI, 15, AND, 1, SHR)]
    c_wgu = ts(T.wgu[:, :], T.wgo[:, :], T.bf[:, 0:1], A.add, i_wgo, c_bf)
    cb += [ts(T.bi[:, 5:6], PI, 7, AND), ts2(T.bi[:, 6:7], PI, 3, SHR, 1, AND)]
    c_m8 = [run("v", lambda: V.memset(T.m8[:, 0:128:8], 0.0), c_m8), run("v", lambda: V.memset(T.pm[:, 0:8], 0.0))]
    c_bf = cp("v", T.bf[:, 2:7], T.bi[:, 2:7], cb)

    k_wr = [cp("sv"[h], T.wr[:, 256 * h:256 * h + 256], T.wgs[:, 0:32].indirect(T.wgu[:, 16 * h:16 * h + 16]), ("dwg", 16), c_wgu) for h in range(2)]
    k_qx = [quant(T.qx, T.sx, 0, 128, T.xs[:, 0:512], ("dx0", 16)), quant(T.qr, T.sr, 0, 128, T.wr[:, :], k_wr)]
    c_meq = ts(T.meq[:, :], T.col[:, 0:128], R, A.is_equal, i_col)
    k_qx = [k_qx, quant(T.qx, T.sx, 128, 128, T.xs[:, 512:1024], ("dx1", 16))]
    Z, Z2 = [[T.ps[:, 512 * (b - h):512 * (b - h) + 128] for h in range(2)] for b in (7, 5)]
    k_z, k_z2 = zip(*[[product(out[h], T.qr, T.sr, 0, T.qx, T.sx, 128 * h, 128, k_qx[h]) for out in (Z, Z2)] for h in range(2)])
    c_e = act(EF, H16, F.Identity, STEP / 16, T.bf[:, 2:3], c_bf)
    c_ro = act(T.bp[:, 3:4], T.bf[:, 5:6], F.Identity, 16.0, T.bf[:, 6:7])
    c_sel = act(T.bp[:, 6:7], T.bf[:, 4:5], F.Relu, -32.0, 64.0)
    c_bp = act(T.bp[:, 2:3], EF, F.Identity, float(B2), float(B2 * (1 + FIRST) - SH), c_e)
    c_k3 = [act(T.bp[:, 4:5], R, F.Identity, 8.0, EF), act(T.bp[:, 5:6], EF, F.Sign, 1.0, float(FIRST))]
    c_sel = act(T.bp[:, 1:2], T.bp[:, 6:7], F.Identity, -1.0, 64.0, c_sel)

    half = lambda t, h, o=0: t[:, o + 128 * h:o + 128 * h + 128]
    c_mne = act(T.mne[:, :], T.meq[:, :], F.Identity, -1.0, 1.0, c_meq)
    k_ulp = [act(half(T.ulp, 0), Z2[0], F.Abs, ULP, TINY, k_z2[0])]
    k_zc = [cp("s", half(T.zz, h), Z2[h], k_z2[h]) for h in range(2)]
    k_ulp.append(act(half(T.ulp, 1), Z2[1], F.Abs, ULP, TINY))
    k = tt(half(T.m1, 0), Z[0], T.meq[:, :], A.mult, k_z[0], c_meq)
    k_fs = [scan(half(T.fs, 0), T.mne[:, :], half(T.m1, 0), A.add, k, c_mne)]
    k = tt(half(T.m1, 1), Z[1], T.meq[:, :], A.mult, k_z[1])
    k_zn = [tt(half(T.zz, 0, 256), Z[0], half(T.ulp, 0), A.add, k_ulp[0])]
    k_fs.append(scan(half(T.fs, 1), T.mne[:, :], half(T.m1, 1), A.add, k))
    k_zn.append(tt(half(T.zz, 1, 256), Z[1], half(T.ulp, 1), A.add, k_ulp[1]))
    k_eq = [tt(half(T.eq, h), Z[h], half(T.fs, h), A.is_equal, k_fs[h]) for h in range(2)]
    own = lambda i: T.fs[:, 16 * i + 15:16 * i + 16]
    row = lambda t, i, n: t[:, SEG * i:SEG * i + n]
    window = lambda i: T.zz[:, 16 * i + 16:16 * i + 272]
    k_cmp = {}

    def compare(*cols):
        for i in cols:
            k_cmp[i] = ts2(row(T.cm, i, 256), window(i), own(i), A.is_gt, -1.0, A.mult, k_fs, k_zc, k_zn)

    def count(i, n):
        return scan(row(T.cv, i - NS, SEG * n), T.msk[:, 0:SEG * n], row(T.cm, i, SEG * n), A.subtract, k_cmp[i + n - 1], k_ext, c_low, c_msk)

    k_eqs = [scan(half(T.eqs, 0), T.mne[:, :], half(T.eq, 0), A.add, k_eq[0])]
    compare(8)
    k_eqs.append(scan(half(T.eqs, 1), T.mne[:, :], half(T.eq, 1), A.add, k_eq[1]))
    compare(9)
    k_ext = ts(T.cm[:, 256:16 * SEG:SEG], T.eqs[:, 15:256:16], -float(SH), A.add, k_eqs)
    compare(10, 11, 12)
    count(8, 3)
    compare(13, 14, 15)
    count(11, 3)
    k_cv = count(14, 2)
    counts = T.cv[:, SEG - 1:(16 - NS) * SEG:SEG]
    turn = list(range(LATE, NS)) + list(range(LATE))
    k_sg = {i: act(row(T.cm, i, 256), window(i), F.Sign, -1.0, own(i), k_fs[0], k_zc, k_zn[0]) for i in turn}
    k_acc = {i: run("s", lambda: S.activation(row(T.cm, i, 257), row(T.cm, i, 257), F.Relu, scale=-1.0, accum_out=T.acc[:, i:i + 1]), k_sg[i], k_ext) for i in turn}
    k_rku = [cp("v", T.rku[:, 0:NS - LATE], T.acc[:, LATE:NS], k_acc[NS - 1]), ts(T.rku[:, NS - LATE:16 - LATE], counts, float(LOW), A.add, k_cv)]
    c_sel = ts(T.selc[:, 0:1], T.bp[:, 1:2], H16, A.add, c_sel)
    k_wa = cp("v", T.wa[:, :].indirect(T.rku[:, :]), T.val[:, 16 * LATE:256], k_rku, i_val)
    k_rku = cp("v", T.rkl[:, :], T.acc[:, 0:LATE], k_acc[LATE - 1])
    c_k3 = ts2(T.selc[:, 2:3], T.bp[:, 4:5], float(FIRST + 7), A.add, T.bp[:, 5:6], A.mult, c_k3)
    k_wa = cp("v", T.wa[:, :].indirect(T.rkl[:, :]), T.val[:, 0:16 * LATE], k_rku, k_wa)

    def spread(src, O, pk, kc, qs):
        ks = [[], []]
        for j in range(4):
            for h in range(2):
                q = 2 * h + j // 2
                d = q ^ (j & 1)
                ks[h].append(cp(qs[j][h], O[32 * d:32 * d + 32, q ^ pk, :], src(q), kc))
            yield
        for h in range(2):
            o = 2 * (h ^ (pk >> 1))
            ks[h].append(cp(qs[4][h], O[64 * (1 - h):64 * (1 - h) + 64, o:o + 2, :], O[64 * h:64 * h + 64, o:o + 2, :], ks[h]))
        yield ks

    k = act(T.acc[:, NS:16], counts, F.Identity, 1.0, float(LOW), k_cv)
    k_tk = act(T.tk[:, :], T.acc[:, :], F.Relu, -BIG, BIG * (CK + SH), k)
    k_pb = act(T.pb[:, :], T.acc[:, :], F.Identity, 1.0, T.bp[:, 2:3], c_bp)
    k_d2 = tt(T.d2[:, :], T.tk[:, :], T.pb[:, :], A.min, k_tk, k_pb)
    ks = [cp("vs"[h], T.wb[:, :, 16 * h:16 * h + 16], T.wa[:, SH:SH + CK], k_wa) for h in range(2)]
    k_va = run("v", lambda: V.transpose(T.va[:, :], T.wb[:, :, :]), ks)
    c_ro = ts(T.rou[:, :], T.ro[:, :], T.bp[:, 3:4], A.add, c_ro, i_ro)
    need("y", k_d2)
    for j in range(16):
        e, p = j // 4 + FIRST + STEP * (j // 2 % 2), 16 * (j % 2)
        g.sync.dma_start(T.tp[p:p + 16, 16 * e:16 * e + 16], T.d2[16 * (j // 2):16 * (j // 2) + 16, :]).then_inc(T.sem.dt, 16)

    q0 = (rank ^ first) & 3
    k_of0 = [ts(T.of[32 * d:32 * d + 32, 0:3], T.va[32 * q0:32 * q0 + 32, 16:96:32], 4.0, A.mult, k_va) for d in range(4)]
    pk = (rank & 3) ^ 3

    def pair(x):
        return [cp("s", T.oa[32 * d:32 * d + 32, y, :], T.va[32 * (y ^ pk):32 * (y ^ pk) + 32, 0:96:16], k_va) for y in (2 * x, 2 * x + 1) for d in (y ^ pk, y ^ pk ^ 1)]

    def offsets(o, y, n, h, *deps):
        p = 64 * ((y ^ pk) >> 1)
        return [ts(T.of[64 * d:64 * d + 64, o:o + 3 * n], T.oa[p:p + 64, y:y + n, h:6:2], 4.0, A.mult, *deps) for d in range(2)]

    k_oa = pair(0)
    win = [T.xs[:, :]] + [T["xs%d" % t][:, 16:16 + 4 * TOK - 3] for t in range(1, 4)]

    def gather(a, n, o, k, qs="vvss"):
        return [cp(qs[t], T.xt[:, 4 * a + t:4 * (a + n):4], win[t].indirect(T.of[:, o:o + n // 16]), k, ("dxs", 48)) for t in (2, 0, 3, 1)]

    def tile(j, ks):
        a, b = TILES[j]
        return quant(T.sb, T.ss, b, 128, T.xt[:, 4 * a:4 * a + 512], ks)

    sent = []

    def send(w, src_col, dst_col, codes, plane, sem, k):
        need("p", k)
        for view in ("q", "s"):
            tr = []
            for j, de in enumerate(waves[w]):
                dst = T.cores[rank ^ de]
                eng = topo.engines(core, dst)
                per = len(eng) // len(waves[w])
                rid, pid = topo.addr(dst, core)
                a, b = src_col[w] + CK * j, dst_col[w] + CK * j
                if view == "q":
                    sa, da = codes[:, a:a + CK].bitcast(dt.uint8), codes[:, b:b + CK].bitcast(dt.uint8)
                else:
                    sa, da = plane[:, a:a + CK], plane[:, b:b + CK]
                tr.append(RemoteDMATransfer(dst_ids=[DstId(rid=rid, pnc=pid)], dma_engine_mask=sum(1 << e for e in eng[per * j:per * j + per]),
                                            remote_sem=T.sem[sem + str(w)], src=sa, dst=da))
            g.remote_dma_fused(tr, local_sem=T.sem.loc)
            sent.append(len(eng))
        return k

    k = gather(128, CK, 0, k_of0)
    k_of = offsets(4, 0, 2, 0, k_oa)
    k_oa = pair(1)
    K = {"tile0": tile(0, [k, c_xt])}
    k = gather(176, 2 * CK, 4, k_of)
    k_of = offsets(10, 2, 2, 0, k_oa)
    k_near = [offsets(16, waves[3][0] ^ 3, 1, 1)]
    K["tile1"] = tile(1, k)
    k_near.append(offsets(19, waves[3][1] ^ 3, 1, 1))
    k = gather(272, 2 * CK, 10, k_of)
    k_own = offsets(22, 3, 1, 1)
    K["tile2"] = tile(2, k)
    for w in range(3):
        send(w, OUT1, IN1, T.sb, T.ss, "a", K["tile%d" % w])
    WAVE = sent[0] + sent[1]

    free, done, k_p = {}, {}, {}
    order = [e for exps in decoded for e in exps]

    def mul(c):
        a, n, o, lo, hi, j = EXPERT[c]
        ks = []
        for i in range(4):
            bank = (4 * c + i) % 8
            k = product(T.ps[:, 512 * bank:512 * bank + n], T.qw, T.sw, i, T.sb, T.ss, a, n, ("a%d" % c, WAVE), K["wa" if i < 2 else "wb"], K["tile%d" % j], k_rku, free.get(bank))
            out, src = T.ht[:, c, 4 * lo + i:4 * hi:4], T.ps[:, 512 * bank + lo:512 * bank + hi]
            ks.append(act(out, src, F.Relu, 0.05, 0.0, k) if RELU[c][i] == "s" else ts2(out, src, 0.0, A.max, 0.05, A.mult, k))
            free[bank] = ks[i]
        return ks

    def back(c):
        a, n, o, lo, hi, j = EXPERT[c]
        return send(c, OUT2, IN2, T.rb, T.rs, "b", quant(T.rb, T.rs, o, n, T.ht[:, c, 0:4 * n], K["mul%d" % c], c_ht))

    def decode(c):
        exps = decoded[c]
        lo, m = order.index(exps[0]), CK * len(exps)
        a, n, last = DECODE[c]
        banks = [(4 * c + b) % 8 for b in range(4)]
        k_d = [product(T.ps[:, 512 * banks[b]:512 * banks[b] + n], T.qe, T.se, b, T.rb, T.rs, a, n,
                       [("b%d" % w, WAVE) for w in range(last + 1)], K["ea"], K["eb"], free[banks[b]], K["back2"] if c else None) for b in range(4)]
        runs = [(j, j + 1) for j in sorted(range(2), key=lambda j: exps[j])] if c == 2 else [(0, len(exps))]
        if c < 2 and 0 in exps:
            j = exps.index(0)
            runs = [(j, j + 1), (int(j == 0), len(exps) - (j == len(exps) - 1))]
        ks = {}
        for x, b in LAST if c == 2 else [(x, b) for x in range(len(runs)) for b in range(4)]:
            (j0, j1), o = runs[x], 512 * banks[b] + n - m
            if exps[j0:j1] == [0]:
                out = T["pp%d" % (b // 2)][:, B2 + CK * (b % 2):B2 + CK * (b % 2) + CK]
            else:
                out = T.vv[:, lo + j0:lo + j1, CK * b:CK * b + CK]
            ks[x, b] = free[banks[b]] = cp(COPY[c][b], out, T.ps[:, o + CK * j0:o + CK * j1], k_d[b])
        for x, (j0, j1) in enumerate(runs):
            for e in exps[j0:j1]:
                done.setdefault(e, [[ks[x, 0], ks[x, 1]], [ks[x, 2], ks[x, 3]]])

    def adds():
        for e in range(len(k_p) // 2, N):
            if e not in done:
                break
            for h in range(2):
                P = T["pp%d" % h]
                k_p[(e, h)] = done[0][h] if e == 0 else tt(
                    P[:, B2 * (e + 1):B2 * (e + 2)], P[:, 0:B2 * (e + 1)].indirect(T.po[:, e, :]), T.vv[:, order.index(e), B2 * h:B2 * h + B2],
                    A.add, k_p[(e - 1, h)], done[e][h], K["final"], K["zeros"])

    def own_lists():
        K["tile4"] = tile(4, K["own"])
        return cp("v", T.sel[:, :], T.va[:, :].indirect(T.selc[:, 0:1]), c_sel)

    step = {
        "near": lambda: gather(368, 2 * CK, 16, k_near, "ssss"),
        "own": lambda: gather(0, CK, 22, k_own, "ssss"),
        "zeros": lambda: [run("s", lambda: S.activation(P[:, 0:B2], T.col[:, 0:B2], F.Copy, scale=0.0), i_col) for P in (T.pp0, T.pp1)],
        "wa": lambda: quant(T.qw, T.sw, 0, 256, T.w1s[:, 0:1024], ("dw1", 16)),
        "wb": lambda: quant(T.qw, T.sw, 256, 256, T.w1s[:, 1024:2048]),
        "ea": lambda: [quant(T.qe, T.se, 128 * b, 128, T.em[:, b, 2:514], i_em) for b in range(2)],
        "eb": lambda: [quant(T.qe, T.se, 256 + 128 * b, 128, T.em[:, b, 0:512], i_em) for b in range(2)],
        "send3": lambda: send(3, OUT1, IN1, T.sb, T.ss, "a", tile(3, K["near"])),
        "lists": own_lists, "adds": adds,
        "half": lambda: cp("v", T.tp[32:64, :], T.tp[0:32, :], ("dt", 256)),
        "whole": lambda: cp("v", T.tp[64:128, :], T.tp[0:64, :], K["half"]),
        "places": lambda: cp("s", T.tq[:, :], T.tp[:, :].indirect(T.rou[:, :]), c_ro, K["whole"]),
        "run": lambda: scan(T.pm[:, 8:136], T.m8[:, :], T.tq[:, :], A.max, K["places"], c_m8),
        "before": lambda: cp("v", T.k3[:, :], T.pm[:, :].indirect(T.selc[:, 2:3]), K["run"], c_k3),
        "last": lambda: [ts(T.lb[:, 16 * b:16 * b + 16], T.pm[:, 15:136:8], float(CK * b), A.add, K["run"]) for b in range(2)],
        "row": lambda: cp("s", T.row[:, :], T.idw[:, :].indirect(T.k3[:, :]), K["before"], i_idw),
        "slots": lambda: cp("s", T.wd[:, :], T.row[:, :].indirect(T.sel[:, 0:6]), K["row"], K["lists"]),
        "turn": lambda: run("v", lambda: V.transpose(T.vc[:, :], T.wd[:, :]), K["slots"]),
        "spread": lambda: list(spread(lambda q: T.vc[32 * q:32 * q + 32, 0:96:16], T.oc, 0, K["turn"], ("vv",) * 5))[-1],
        "final": lambda: [ts(T.po[:, e:e + 4, 3 * b:3 * b + 3], T.oc[:, :, h:6:2], float(CK * b), A.add, K["spread"])
                          for h, e in ((0, FIRST), (1, FIRST + STEP)) for b in range(2)],
    }
    for name in ORDER.split():
        K[name] = step[name]() if name in step else {"mul": mul, "back": back, "decode": decode}[name[:-1]](int(name[-1]))

    a = 0
    for n in PIECES:
        ks = []
        for b in range(4):
            ks.append(cp("sv"[b % 2], T.yo[:, 64 * a + b:64 * (a + n):4], T["pp%d" % (b // 2)][:, :].indirect(T.lb[:, 16 * (b % 2) + a:16 * (b % 2) + a + n]),
                         k_p[(7, b // 2)], K["last"]))
        need("y", ks)
        g.sync.dma_start(T.y[:, 64 * a:64 * (a + n)], T.yo[:, 64 * a:64 * (a + n)]).then_inc(T.sem.dy, 16)
        a += n
    need("y", ("dy", 16 * len(PIECES)))
    need("p", [("v", cnt["v"]), ("s", cnt["s"]), ("t", cnt["t"]), ("p", cnt["p"]), ("loc", sum(sent))])
